import numpy as np
import ml_dtypes


def mxq(x, axis, fmt="e4m3"):
    dtype, down = {"e4m3": (ml_dtypes.float8_e4m3fn, 7), "e5m2": (ml_dtypes.float8_e5m2, 14)}[fmt]
    v = np.moveaxis(np.asarray(x, np.float32).astype(ml_dtypes.bfloat16).astype(np.float64), axis, -1)
    blocks = v.reshape(v.shape[:-1] + (-1, 32))
    amax = np.abs(blocks).max(-1, keepdims=True)
    byte = np.maximum(np.where(amax > 0, np.frexp(amax)[1] - 1 + 127, 0) - down, 1)
    scale = np.exp2(byte - 127.0)
    codes = (blocks / scale).astype(np.float32).astype(dtype).astype(np.float64)
    return np.moveaxis((codes * scale).reshape(v.shape), -1, axis)


WIDE = False


def mx_kscale(k):
    if not WIDE:
        return np.ones(k)
    levels = np.array([10, -10, 5, -5, 0])
    if k % 512:
        return np.exp2(np.random.permutation(np.resize(levels, k // 32))).repeat(32)
    a = np.empty((k // 512, 16))
    for p in range(k // 512):
        a[p, :8] = np.random.permutation(np.resize(levels, 8))
        for g in range(8):
            far = levels[np.abs(levels - a[p, g]) >= 10]
            a[p, g + 8] = far[np.random.randint(len(far))]
    return np.exp2(a.ravel()).repeat(32)


def f64(x):
    return np.asarray(x).astype(np.float64)


def striped(idx):
    return np.tile(idx.reshape(-1, 16).T, (8, 1)).astype(np.uint16)


def unstriped(offs):
    return offs[:16].T.reshape(-1).astype(np.int64)


def striped8(idx):
    return np.concatenate([x.reshape(-1, 16).T for x in idx]).astype(np.uint16)


def runs(offs, k):
    lists = np.stack([offs[16 * r : 16 * r + 16].T.reshape(-1) for r in range(8)]).astype(np.int64)
    return lists[np.arange(k) % 512 // 64]


def pack_weight(w):
    k, n = w.shape
    w = f64(np.asarray(w, np.float32).astype(ml_dtypes.bfloat16)).reshape(k // 32, 32, n)
    amax = np.abs(w).max(1)
    byte = np.clip(np.where(amax > 0, np.frexp(amax)[1] - 1 + 127 - 7, 1), 1, 254)
    scaled = (w * np.exp2(127.0 - byte)[:, None, :]).reshape(k, n).astype(np.float32)
    words = np.ascontiguousarray(scaled.reshape(k // 512, 128, 4, n).transpose(0, 1, 3, 2)).astype(ml_dtypes.float8_e4m3fn).view(np.uint8)
    return words, np.ascontiguousarray(byte.astype(np.uint8).reshape(k // 512, 16, n))


def unpack_weight(words, scales):
    g, p, n, _ = words.shape
    vals = np.ascontiguousarray(words).view(ml_dtypes.float8_e4m3fn).astype(np.float64) * np.repeat(np.exp2(scales.astype(np.float64) - 127.0), 8, axis=1)[..., None]
    return vals.transpose(0, 1, 3, 2).reshape(g * 512, n)


def gelu(v):
    return 0.5 * v * (1.0 + np.tanh(np.sqrt(2.0 / np.pi) * (v + 0.044715 * v**3)))

def planes(y):
    n, m = y.shape
    v = y.astype(np.float32).astype(ml_dtypes.bfloat16).astype(np.float64).reshape(n // 32, 32, m)
    top = np.abs(v).max(1)
    byte = np.clip(np.where(top > 0, np.frexp(top)[1] - 1 + 127 - 7, 1), 1, 254)
    codes = (v * np.exp2(127.0 - byte)[:, None, :]).reshape(n, m).astype(np.float32).astype(ml_dtypes.float8_e4m3fn).view(np.uint8)
    words = codes.reshape(n // 512, 128, 4, m).transpose(0, 1, 3, 2)
    return np.ascontiguousarray(words), np.ascontiguousarray(byte.astype(np.uint8).reshape(n // 512, 16, m))


K, T, S, N, H, U = 512, 2048, 512, 512, 512, 1024


def setup_inputs():
    n = np.random.standard_normal
    s = mx_kscale(K)[:, None]
    u = mx_kscale(H)
    packed_xT = pack_weight(n((K, T)) * s)
    packed_w1 = pack_weight(n((K, H)) / np.sqrt(K) / s)
    packed_w2 = pack_weight(n((H, N)) / np.sqrt(H) / u[:, None])
    return {
        "x_words": packed_xT[0],
        "x_scales": packed_xT[1],
        "w1_words": packed_w1[0],
        "w1_scales": packed_w1[1],
        "gamma": (np.random.uniform(0.5, 1.5, (H, U)) * u[:, None]).astype(np.float32),
        "beta": (n((H, U)) * u[:, None]).astype(np.float32),
        "w2_words": packed_w2[0],
        "w2_scales": packed_w2[1],
        "offs": striped(np.random.permutation(T)[:S]),
        "sty": striped8(np.random.randint(0, U, (8, S))),
    }


def reference(x_words, x_scales, w1_words, w1_scales, gamma, beta, w2_words, w2_scales, offs, sty):
    xq = unpack_weight(x_words, x_scales)[:, unstriped(offs)]
    y = unpack_weight(w1_words, w1_scales).T @ xq
    h = (y - y.mean(axis=1, keepdims=True)) / np.sqrt(y.var(axis=1, keepdims=True) + 1e-5)
    z = gelu(h * (f64(gamma)[np.arange(H)[:, None], runs(sty, H)]) + f64(beta)[np.arange(H)[:, None], runs(sty, H)])
    out_0 = unpack_weight(w2_words, w2_scales).T @ mxq(z, 0, "e4m3")
    return (out_0,) + planes(out_0)

@@ -1,0 +1,184 @@
+from contextlib import ExitStack
+
+import concourse.mybir as mybir
+
+K, T, S, H, N, U = 512, 2048, 512, 512, 512, 1024
+FLOPS = 2 * K * H * S + 2 * H * N * S
+
+F32 = mybir.dt.float32
+BF16 = mybir.dt.bfloat16
+I32 = mybir.dt.int32
+U32 = mybir.dt.uint32
+U16 = mybir.dt.uint16
+U8 = mybir.dt.uint8
+FP8X4 = mybir.dt.float8_e4m3fn_x4
+ACT = mybir.ActivationFunctionType
+ALU = mybir.AluOpType
+
+P = 128
+PACK = 4
+HALF = 256
+CHUNK = 128
+EPS = 1e-5
+
+
+def tile_picked_adain8_gelu_po_kernel(
+    tc, x_words, x_scales, w1_words, w1_scales, gamma, beta, w2_words, w2_scales, offs, sty, out_0, out_1, out_2
+):
+    nc = tc.nc
+
+    def words_of(dram):
+        return dram[0].rearrange("p n t -> p (n t)").bitcast(I32)
+
+    with ExitStack() as ctx:
+        keep = ctx.enter_context(tc.tile_pool(name="keep", bufs=1))
+        psum = ctx.enter_context(tc.psum_pool(name="psum", bufs=1))
+
+        offs_sb = keep.tile([P, S // 16], U16, name="offs_sb")
+        sty_sb = keep.tile([P, S // 16], U16, name="sty_sb")
+        x_w = keep.tile([P, T], U32, name="x_w", tag="x_w", align_bytes=64)
+        x_s = keep.tile([P, T], U8, name="x_s", align_bytes=64)
+        w1_w = keep.tile([P, H], U32, name="w1_w", align_bytes=64)
+        w2_w = keep.tile([P, N], U32, name="w2_w", align_bytes=64)
+        w1_s = keep.tile([P, H], U8, name="w1_s", tag="w1_s", align_bytes=64)
+        w2_s = keep.tile([P, N], U8, name="w2_s", align_bytes=64)
+        g_sb = [keep.tile([P, U], F32, name="g_sb%d" % t) for t in range(PACK)]
+        b_sb = [keep.tile([P, U], F32, name="b_sb%d" % t) for t in range(PACK)]
+
+        nc.gpsimd.memset(x_s[:, T // 2 :].bitcast(I32), 0)
+        nc.vector.memset(x_s[:, : T // 2].bitcast(I32), 0)
+        nc.vector.memset(w1_s[:].bitcast(I32), 0)
+        nc.gpsimd.memset(w2_s[:].bitcast(I32), 0)
+
+        warm = keep.tile([P, 2], F32, name="warm")
+        nc.gpsimd.memset(warm[:, 0:1], 1.0)
+        nc.scalar.activation(warm[:, 1:2], warm[:, 0:1], ACT.Abs_reciprocal_sqrt, bias=EPS)
+
+        g_rows = gamma.rearrange("(p t) u -> p t u", t=PACK)
+        b_rows = beta.rearrange("(p t) u -> p t u", t=PACK)
+
+        def load_scales(engines, tile, dram):
+            for q in range(4):
+                engines[q].dma_start(out=tile[32 * q : 32 * q + 4, :].bitcast(I32), in_=dram[0, 4 * q : 4 * q + 4, :].bitcast(I32))
+
+        nc.sync.dma_start(offs_sb[:], offs)
+        load_scales([nc.sync, nc.scalar, nc.sync, nc.scalar], x_s, x_scales)
+        nc.scalar.dma_start(out=w1_w[:].bitcast(I32), in_=words_of(w1_words))
+        nc.sync.dma_start(out=x_w[:].bitcast(I32), in_=words_of(x_words))
+        load_scales([nc.sync] * 4, w1_s, w1_scales)
+        nc.sync.dma_start(out=w2_w[:].bitcast(I32), in_=words_of(w2_words))
+        nc.sync.dma_start(out=g_sb[0][:], in_=g_rows[:, 0, :])
+        nc.sync.dma_start(sty_sb[:], sty)
+        nc.sync.dma_start(out=g_sb[1][:], in_=g_rows[:, 1, :])
+        nc.sync.dma_start(out=b_sb[0][:], in_=b_rows[:, 0, :])
+        load_scales([nc.sync] * 4, w2_s, w2_scales)
+        nc.sync.dma_start(out=b_sb[1][:], in_=b_rows[:, 1, :])
+        for t in (2, 3):
+            nc.sync.dma_start(out=g_sb[t][:], in_=g_rows[:, t, :])
+        for t in (2, 3):
+            nc.sync.dma_start(out=b_sb[t][:], in_=b_rows[:, t, :])
+
+        xg_w = keep.tile([P, S], U32, name="xg_w", align_bytes=64)
+        xg_s = keep.tile([P, S], U8, name="xg_s", align_bytes=64)
+
+        w1_d = keep.tile([P, H], U32, name="w1_d", align_bytes=64)
+
+        def deal(dst, src):
+            nc.vector.tensor_copy(out=dst[:].rearrange("p (t m) -> p m t", t=PACK), in_=src[:].rearrange("p (m t) -> p m t", t=PACK))
+
+        nc.vector.tensor_copy(xg_s[:], x_s[:].indirect(offs_sb[:]))
+        deal(w1_d, w1_w)
+        nc.vector.tensor_copy(xg_w[:], x_w[:].indirect(offs_sb[:]))
+        w1s_d = keep.tile([P, H], U8, name="w1s_d", tag="x_w", align_bytes=64)
+        deal(w1s_d, w1_s)
+        w2_d = keep.tile([P, N], U32, name="w2_d", tag="w1_s", align_bytes=64)
+        deal(w2_d, w2_w)
+
+        h_sb = []
+        for t in range(PACK):
+            cols = slice(t * P, (t + 1) * P)
+            y = psum.tile([P, S], F32, name="y%d" % t)
+            nc.tensor.matmul_mx(
+                out=y[:], lhsT=w1_d[:, cols].bitcast(FP8X4), lhsT_scale=w1s_d[:, cols],
+                rhs=xg_w[:].bitcast(FP8X4), rhs_scale=xg_s[:], start=True, stop=True,
+            )
+            neg_mean = keep.tile([P, 1], F32, name="neg_mean%d" % t)
+            rstd = keep.tile([P, 1], F32, name="rstd%d" % t)
+            shift = keep.tile([P, 1], F32, name="shift%d" % t)
+            h = keep.tile([P, S], F32, name="h%d" % t)
+            stats = keep.tile([P, 6], F32, name="stats%d" % t, tag="stats%d" % max(t, 1))
+            mv = keep.tile([P, 2], F32, name="mv%d" % t)
+            nc.vector.bn_stats(stats[:], y[:])
+            nc.vector.bn_aggr(mv[:], stats[:])
+            nc.scalar.activation(rstd[:], mv[:, 1:2], ACT.Abs_reciprocal_sqrt, bias=EPS)
+            nc.scalar.activation(neg_mean[:], mv[:, 0:1], ACT.Identity, scale=-1.0)
+            nc.scalar.activation(shift[:], neg_mean[:], ACT.Identity, scale=rstd[:])
+            nc.scalar.activation(h[:], y[:], ACT.Identity, bias=shift[:], scale=rstd[:])
+            h_sb.append(h)
+
+        out_rows = out_0.rearrange("(p t) j -> p t j", t=PACK)
+        out_words = out_1[0].rearrange("p n t -> p (n t)").bitcast(I32)
+        o_s = keep.tile([P, S], U8, name="o_s", align_bytes=64)
+        z_sb = [keep.tile([P, CHUNK, PACK], BF16, name="z%d" % c, tag="z%d" % c, align_bytes=64) for c in range(S // CHUNK)]
+
+        def modulate(pair, first, width, u_tag):
+            cols = slice(first, first + width)
+            lists = sty_sb[:, first // 16 : (first + width) // 16]
+            scaled = keep.tile([P, 2, width], F32, name="scaled%d_%d" % (pair, first), tag="scaled%d" % pair, align_bytes=64)
+            for e in range(2):
+                t = 2 * pair + e
+                nc.vector.tensor_tensor(scaled[:, e, :], g_sb[t][:].indirect(lists), h_sb[t][:, cols], ALU.mult)
+            u = keep.tile([P, 2, width], F32, name="u%d_%d" % (pair, first), tag=u_tag, align_bytes=64)
+            for e in range(2):
+                t = 2 * pair + e
+                nc.vector.tensor_tensor(u[:, e, :], b_sb[t][:].indirect(lists), scaled[:, e, :], ALU.add)
+            for cc in range(width // CHUNK):
+                nc.scalar.activation(
+                    z_sb[first // CHUNK + cc][:, :, 2 * pair : 2 * pair + 2],
+                    u[:, :, cc * CHUNK : (cc + 1) * CHUNK].rearrange("p e j -> p j e"),
+                    ACT.Gelu_apprx_tanh,
+                )
+
+        def second_product(c):
+            z_w = keep.tile([P, CHUNK], U32, name="z_w%d" % c, align_bytes=64)
+            z_s = keep.tile([P, CHUNK], U8, name="z_s%d" % c, align_bytes=64)
+            nc.vector.quantize_mx(out=z_w[:].bitcast(FP8X4), scales=z_s[:], in_=z_sb[c][:].rearrange("p j t -> p (j t)"))
+            acc = psum.tile([P, PACK, CHUNK], F32, name="acc%d" % c)
+            for t in range(PACK):
+                wc = slice(t * P, (t + 1) * P)
+                nc.tensor.matmul_mx(
+                    out=acc[:, t, :], lhsT=w2_d[:, wc].bitcast(FP8X4), lhsT_scale=w2s_d[:, wc],
+                    rhs=z_w[:].bitcast(FP8X4), rhs_scale=z_s[:], start=True, stop=True,
+                )
+            return acc
+
+        def hand_out(c, acc, o_w):
+            ccols = slice(c * CHUNK, (c + 1) * CHUNK)
+            o32 = keep.tile([P, PACK, CHUNK], F32, name="o32_%d" % c)
+            o16 = keep.tile([P, CHUNK, PACK], BF16, name="o16_%d" % c, align_bytes=64)
+            if c == 0:
+                nc.vector.tensor_copy(o32[:], acc[:])
+            else:
+                nc.scalar.copy(o32[:], acc[:])
+            nc.sync.dma_start(out=out_rows[:, :, ccols], in_=o32[:])
+            nc.vector.tensor_copy(o16[:], o32[:].rearrange("p t j -> p j t"))
+            nc.vector.quantize_mx(
+                out=o_w[:, (c % 2) * CHUNK : (c % 2 + 1) * CHUNK].bitcast(FP8X4), scales=o_s[:, ccols],
+                in_=o16[:].rearrange("p j t -> p (j t)"),
+            )
+
+        modulate(0, 0, S, "u_low")
+        w2s_d = keep.tile([P, N], U8, name="w2s_d", tag="scaled0", align_bytes=64)
+        deal(w2s_d, w2_s)
+        modulate(1, 0, HALF, "u_first")
+        accs = [second_product(0), second_product(1)]
+        modulate(1, HALF, HALF, "z1")
+        accs = accs + [second_product(2), second_product(3)]
+        for half in range(2):
+            o_w = keep.tile([P, HALF], U32, name="o_w%d" % half, align_bytes=64)
+            for c in (2 * half, 2 * half + 1):
+                hand_out(c, accs[c], o_w)
+            nc.sync.dma_start(out=out_words[:, half * HALF : (half + 1) * HALF], in_=o_w[:].bitcast(I32))
+        for q in range(4):
+            eng = nc.scalar if q % 2 else nc.sync
+            eng.dma_start(out=out_2[0, 4 * q : 4 * q + 4, :].bitcast(I32), in_=o_s[32 * q : 32 * q + 4, :].bitcast(I32))

@@ -94,41 +94,58 @@ def tile_picked_adain8_gelu_po_kernel(
         w2_d = keep.tile([P, N], U32, name="w2_d", tag="w1_s", align_bytes=64)
         deal(w2_d, w2_w)
 
-        h_sb = []
-        for t in range(PACK):
+        y_ps, moments, rstd, neg_mean, shift, h_sb = [], [], [], [], [], []
+
+        def first_product(t):
             cols = slice(t * P, (t + 1) * P)
-            y = psum.tile([P, S], F32, name="y%d" % t)
+            y = psum.tile([P, S], F32, name="y%d" % t, tag="y%d" % t)
             nc.tensor.matmul_mx(
                 out=y[:], lhsT=w1_d[:, cols].bitcast(FP8X4), lhsT_scale=w1s_d[:, cols],
                 rhs=xg_w[:].bitcast(FP8X4), rhs_scale=xg_s[:], start=True, stop=True,
             )
-            neg_mean = keep.tile([P, 1], F32, name="neg_mean%d" % t)
-            rstd = keep.tile([P, 1], F32, name="rstd%d" % t)
-            shift = keep.tile([P, 1], F32, name="shift%d" % t)
-            h = keep.tile([P, S], F32, name="h%d" % t)
-            stats = keep.tile([P, 6], F32, name="stats%d" % t, tag="stats%d" % max(t, 1))
-            mv = keep.tile([P, 2], F32, name="mv%d" % t)
+            stats = keep.tile([P, 6], F32, name="stats%d" % t)
+            mv = keep.tile([P, 2], F32, name="mv%d" % t, tag="mv%d" % t)
             nc.vector.bn_stats(stats[:], y[:])
             nc.vector.bn_aggr(mv[:], stats[:])
-            nc.scalar.activation(rstd[:], mv[:, 1:2], ACT.Abs_reciprocal_sqrt, bias=EPS)
-            nc.scalar.activation(neg_mean[:], mv[:, 0:1], ACT.Identity, scale=-1.0)
-            nc.scalar.activation(shift[:], neg_mean[:], ACT.Identity, scale=rstd[:])
-            nc.scalar.activation(h[:], y[:], ACT.Identity, bias=shift[:], scale=rstd[:])
-            h_sb.append(h)
+            y_ps.append(y)
+            moments.append(mv)
+
+        def scale_of(t):
+            rstd.append(keep.tile([P, 1], F32, name="rstd%d" % t))
+            neg_mean.append(keep.tile([P, 1], F32, name="neg_mean%d" % t))
+            nc.scalar.activation(rstd[t][:], moments[t][:, 1:2], ACT.Abs_reciprocal_sqrt, bias=EPS)
+            nc.scalar.activation(neg_mean[t][:], moments[t][:, 0:1], ACT.Identity, scale=-1.0)
+
+        def shift_of(t):
+            shift.append(keep.tile([P, 1], F32, name="shift%d" % t))
+            nc.scalar.activation(shift[t][:], neg_mean[t][:], ACT.Identity, scale=rstd[t][:])
+
+        def normalise(t):
+            h_sb.append(keep.tile([P, S], F32, name="h%d" % t, tag="mv%d" % (t + 1)))
+            nc.scalar.activation(h_sb[t][:], y_ps[t][:], ACT.Identity, bias=shift[t][:], scale=rstd[t][:])
+
+        for t in range(PACK):
+            first_product(t)
+        scale_of(0)
+        for t in range(PACK):
+            shift_of(t)
+            if t + 1 < PACK:
+                scale_of(t + 1)
+            normalise(t)
 
         out_rows = out_0.rearrange("(p t) j -> p t j", t=PACK)
         out_words = out_1[0].rearrange("p n t -> p (n t)").bitcast(I32)
         o_s = keep.tile([P, S], U8, name="o_s", align_bytes=64)
         z_sb = [keep.tile([P, CHUNK, PACK], BF16, name="z%d" % c, tag="z%d" % c, align_bytes=64) for c in range(S // CHUNK)]
 
-        def modulate(pair, first, width, u_tag):
+        def modulate(pair, first, width, product_tag, sum_tag):
             cols = slice(first, first + width)
             lists = sty_sb[:, first // 16 : (first + width) // 16]
-            scaled = keep.tile([P, 2, width], F32, name="scaled%d_%d" % (pair, first), tag="scaled%d" % pair, align_bytes=64)
+            scaled = keep.tile([P, 2, width], F32, name="scaled%d_%d" % (pair, first), tag=product_tag, align_bytes=64)
             for e in range(2):
                 t = 2 * pair + e
                 nc.vector.tensor_tensor(scaled[:, e, :], g_sb[t][:].indirect(lists), h_sb[t][:, cols], ALU.mult)
-            u = keep.tile([P, 2, width], F32, name="u%d_%d" % (pair, first), tag=u_tag, align_bytes=64)
+            u = keep.tile([P, 2, width], F32, name="u%d_%d" % (pair, first), tag=sum_tag, align_bytes=64)
             for e in range(2):
                 t = 2 * pair + e
                 nc.vector.tensor_tensor(u[:, e, :], b_sb[t][:].indirect(lists), scaled[:, e, :], ALU.add)
@@ -143,23 +160,31 @@ def tile_picked_adain8_gelu_po_kernel(
             z_w = keep.tile([P, CHUNK], U32, name="z_w%d" % c, align_bytes=64)
             z_s = keep.tile([P, CHUNK], U8, name="z_s%d" % c, align_bytes=64)
             nc.vector.quantize_mx(out=z_w[:].bitcast(FP8X4), scales=z_s[:], in_=z_sb[c][:].rearrange("p j t -> p (j t)"))
-            acc = psum.tile([P, PACK, CHUNK], F32, name="acc%d" % c)
+            if c < 3:
+                acc = psum.tile([P, PACK, CHUNK], F32, name="acc%d" % c)
+                banks = [acc[:, 0:2, :], acc[:, 2:4, :]]
+            else:
+                low = psum.tile([P, 2, CHUNK], F32, name="acc3_low")
+                high = psum.tile([P, 2, CHUNK], F32, name="acc3_high", tag="y0")
+                acc = None
+                banks = [low[:], high[:]]
             for t in range(PACK):
                 wc = slice(t * P, (t + 1) * P)
                 nc.tensor.matmul_mx(
-                    out=acc[:, t, :], lhsT=w2_d[:, wc].bitcast(FP8X4), lhsT_scale=w2s_d[:, wc],
+                    out=banks[t // 2][:, t % 2, :], lhsT=w2_d[:, wc].bitcast(FP8X4), lhsT_scale=w2s_d[:, wc],
                     rhs=z_w[:].bitcast(FP8X4), rhs_scale=z_s[:], start=True, stop=True,
                 )
-            return acc
+            return acc, banks
 
-        def hand_out(c, acc, o_w):
+        def hand_out(c, acc, banks, o_w):
             ccols = slice(c * CHUNK, (c + 1) * CHUNK)
             o32 = keep.tile([P, PACK, CHUNK], F32, name="o32_%d" % c)
             o16 = keep.tile([P, CHUNK, PACK], BF16, name="o16_%d" % c, align_bytes=64)
-            if c == 0:
-                nc.vector.tensor_copy(o32[:], acc[:])
-            else:
+            if c < 3:
                 nc.scalar.copy(o32[:], acc[:])
+            else:
+                nc.scalar.copy(o32[:, 0:2, :], banks[0])
+                nc.vector.tensor_copy(o32[:, 2:4, :], banks[1])
             nc.sync.dma_start(out=out_rows[:, :, ccols], in_=o32[:])
             nc.vector.tensor_copy(o16[:], o32[:].rearrange("p t j -> p j t"))
             nc.vector.quantize_mx(
@@ -167,18 +192,21 @@ def tile_picked_adain8_gelu_po_kernel(
                 in_=o16[:].rearrange("p j t -> p (j t)"),
             )
 
-        modulate(0, 0, S, "u_low")
+        o_w = [keep.tile([P, HALF], U32, name="o_w%d" % half, align_bytes=64) for half in range(2)]
+
+        modulate(0, 0, S, "scaled0", "u_low")
         w2s_d = keep.tile([P, N], U8, name="w2s_d", tag="scaled0", align_bytes=64)
         deal(w2s_d, w2_s)
-        modulate(1, 0, HALF, "u_first")
-        accs = [second_product(0), second_product(1)]
-        modulate(1, HALF, HALF, "z1")
-        accs = accs + [second_product(2), second_product(3)]
-        for half in range(2):
-            o_w = keep.tile([P, HALF], U32, name="o_w%d" % half, align_bytes=64)
-            for c in (2 * half, 2 * half + 1):
-                hand_out(c, accs[c], o_w)
-            nc.sync.dma_start(out=out_words[:, half * HALF : (half + 1) * HALF], in_=o_w[:].bitcast(I32))
+        modulate(1, 0, HALF, "scaled1", "u_first")
+        products = [second_product(0), second_product(1)]
+        hand_out(0, *products[0], o_w[0])
+        modulate(1, HALF, HALF, "scaled1", "z1")
+        hand_out(1, *products[1], o_w[0])
+        nc.sync.dma_start(out=out_words[:, 0:HALF], in_=o_w[0][:].bitcast(I32))
+        products = [second_product(2), second_product(3)]
+        for c in (2, 3):
+            hand_out(c, *products[c - 2], o_w[1])
+        nc.scalar.dma_start(out=out_words[:, HALF:S], in_=o_w[1][:].bitcast(I32))
         for q in range(4):
             eng = nc.scalar if q % 2 else nc.sync
             eng.dma_start(out=out_2[0, 4 * q : 4 * q + 4, :].bitcast(I32), in_=o_s[32 * q : 32 * q + 4, :].bitcast(I32))

@@ -50,33 +50,33 @@ def tile_picked_adain8_gelu_po_kernel(
         nc.vector.memset(w1_s[:].bitcast(I32), 0)
         nc.gpsimd.memset(w2_s[:].bitcast(I32), 0)
 
-        warm = keep.tile([P, 2], F32, name="warm")
-        nc.gpsimd.memset(warm[:, 0:1], 1.0)
-        nc.scalar.activation(warm[:, 1:2], warm[:, 0:1], ACT.Abs_reciprocal_sqrt, bias=EPS)
-
         g_rows = gamma.rearrange("(p t) u -> p t u", t=PACK)
         b_rows = beta.rearrange("(p t) u -> p t u", t=PACK)
 
         def load_scales(engines, tile, dram):
-            for q in range(4):
-                engines[q].dma_start(out=tile[32 * q : 32 * q + 4, :].bitcast(I32), in_=dram[0, 4 * q : 4 * q + 4, :].bitcast(I32))
+            for r in range(4):
+                engines[r].dma_start(out=tile[r:P:32, :].bitcast(I32), in_=dram[0, r:16:4, :].bitcast(I32))
 
         nc.sync.dma_start(offs_sb[:], offs)
         load_scales([nc.sync, nc.scalar, nc.sync, nc.scalar], x_s, x_scales)
-        nc.scalar.dma_start(out=w1_w[:].bitcast(I32), in_=words_of(w1_words))
+        nc.sync.dma_start(sty_sb[:], sty)
+        nc.sync.dma_start(out=w1_w[:].bitcast(I32), in_=words_of(w1_words))
         nc.sync.dma_start(out=x_w[:].bitcast(I32), in_=words_of(x_words))
         load_scales([nc.sync] * 4, w1_s, w1_scales)
         nc.sync.dma_start(out=w2_w[:].bitcast(I32), in_=words_of(w2_words))
         nc.sync.dma_start(out=g_sb[0][:], in_=g_rows[:, 0, :])
-        nc.sync.dma_start(sty_sb[:], sty)
-        nc.sync.dma_start(out=g_sb[1][:], in_=g_rows[:, 1, :])
-        nc.sync.dma_start(out=b_sb[0][:], in_=b_rows[:, 0, :])
         load_scales([nc.sync] * 4, w2_s, w2_scales)
-        nc.sync.dma_start(out=b_sb[1][:], in_=b_rows[:, 1, :])
+        nc.sync.dma_start(out=g_sb[1][:], in_=g_rows[:, 1, :])
+        for t in (0, 1):
+            nc.sync.dma_start(out=b_sb[t][:], in_=b_rows[:, t, :])
         for t in (2, 3):
             nc.sync.dma_start(out=g_sb[t][:], in_=g_rows[:, t, :])
         for t in (2, 3):
             nc.sync.dma_start(out=b_sb[t][:], in_=b_rows[:, t, :])
+
+        warm = keep.tile([P, 2], F32, name="warm")
+        nc.gpsimd.memset(warm[:, 0:1], 1.0)
+        nc.scalar.activation(warm[:, 1:2], warm[:, 0:1], ACT.Abs_reciprocal_sqrt, bias=EPS)
 
         xg_w = keep.tile([P, S], U32, name="xg_w", align_bytes=64)
         xg_s = keep.tile([P, S], U8, name="xg_s", align_bytes=64)
@@ -103,7 +103,7 @@ def tile_picked_adain8_gelu_po_kernel(
                 out=y[:], lhsT=w1_d[:, cols].bitcast(FP8X4), lhsT_scale=w1s_d[:, cols],
                 rhs=xg_w[:].bitcast(FP8X4), rhs_scale=xg_s[:], start=True, stop=True,
             )
-            stats = keep.tile([P, 6], F32, name="stats%d" % t)
+            stats = keep.tile([P, 6], F32, name="stats%d" % t, tag="stats%d" % t, align_bytes=64)
             mv = keep.tile([P, 2], F32, name="mv%d" % t, tag="mv%d" % t)
             nc.vector.bn_stats(stats[:], y[:])
             nc.vector.bn_aggr(mv[:], stats[:])
@@ -126,6 +126,8 @@ def tile_picked_adain8_gelu_po_kernel(
 
         for t in range(PACK):
             first_product(t)
+        w2s_d = keep.tile([P, N], U8, name="w2s_d", tag="stats3", align_bytes=64)
+        deal(w2s_d, w2_s)
         scale_of(0)
         for t in range(PACK):
             shift_of(t)
@@ -195,17 +197,15 @@ def tile_picked_adain8_gelu_po_kernel(
         o_w = [keep.tile([P, HALF], U32, name="o_w%d" % half, align_bytes=64) for half in range(2)]
 
         modulate(0, 0, S, "scaled0", "u_low")
-        w2s_d = keep.tile([P, N], U8, name="w2s_d", tag="scaled0", align_bytes=64)
-        deal(w2s_d, w2_s)
         modulate(1, 0, HALF, "scaled1", "u_first")
         products = [second_product(0), second_product(1)]
         hand_out(0, *products[0], o_w[0])
         modulate(1, HALF, HALF, "scaled1", "z1")
+        products = products + [second_product(2), second_product(3)]
         hand_out(1, *products[1], o_w[0])
         nc.sync.dma_start(out=out_words[:, 0:HALF], in_=o_w[0][:].bitcast(I32))
-        products = [second_product(2), second_product(3)]
         for c in (2, 3):
-            hand_out(c, *products[c - 2], o_w[1])
+            hand_out(c, *products[c], o_w[1])
         nc.scalar.dma_start(out=out_words[:, HALF:S], in_=o_w[1][:].bitcast(I32))
         for q in range(4):
             eng = nc.scalar if q % 2 else nc.sync

@@ -17,8 +17,12 @@ ALU = mybir.AluOpType
 
 P = 128
 PACK = 4
+GROUP = 16
+QUADRANT = 32
+SCALE_ROWS = 16
 HALF = 256
 CHUNK = 128
+LAST_CHUNK = S // CHUNK - 1
 EPS = 1e-5
 
 
@@ -34,8 +38,8 @@ def tile_picked_adain8_gelu_po_kernel(
         keep = ctx.enter_context(tc.tile_pool(name="keep", bufs=1))
         psum = ctx.enter_context(tc.psum_pool(name="psum", bufs=1))
 
-        offs_sb = keep.tile([P, S // 16], U16, name="offs_sb")
-        sty_sb = keep.tile([P, S // 16], U16, name="sty_sb")
+        offs_sb = keep.tile([P, S // GROUP], U16, name="offs_sb")
+        sty_sb = keep.tile([P, S // GROUP], U16, name="sty_sb")
         x_w = keep.tile([P, T], U32, name="x_w", tag="x_w", align_bytes=64)
         x_s = keep.tile([P, T], U8, name="x_s", align_bytes=64)
         w1_w = keep.tile([P, H], U32, name="w1_w", align_bytes=64)
@@ -45,28 +49,28 @@ def tile_picked_adain8_gelu_po_kernel(
         g_sb = [keep.tile([P, U], F32, name="g_sb%d" % t) for t in range(PACK)]
         b_sb = [keep.tile([P, U], F32, name="b_sb%d" % t) for t in range(PACK)]
 
-        nc.gpsimd.memset(x_s[:, T // 2 :].bitcast(I32), 0)
-        nc.vector.memset(x_s[:, : T // 2].bitcast(I32), 0)
-        nc.vector.memset(w1_s[:].bitcast(I32), 0)
-        nc.gpsimd.memset(w2_s[:].bitcast(I32), 0)
+        for scale_tile in (x_s, w1_s, w2_s):
+            nc.vector.memset(scale_tile[:].bitcast(I32), 0)
 
         g_rows = gamma.rearrange("(p t) u -> p t u", t=PACK)
         b_rows = beta.rearrange("(p t) u -> p t u", t=PACK)
 
         def load_scales(engines, tile, dram):
-            for r in range(4):
-                engines[r].dma_start(out=tile[r:P:32, :].bitcast(I32), in_=dram[0, r:16:4, :].bitcast(I32))
+            for r in range(PACK):
+                engines[r].dma_start(
+                    out=tile[r:P:QUADRANT, :].bitcast(I32), in_=dram[0, r:SCALE_ROWS:PACK, :].bitcast(I32)
+                )
 
         nc.sync.dma_start(offs_sb[:], offs)
         load_scales([nc.sync, nc.scalar, nc.sync, nc.scalar], x_s, x_scales)
         nc.sync.dma_start(sty_sb[:], sty)
         nc.sync.dma_start(out=w1_w[:].bitcast(I32), in_=words_of(w1_words))
         nc.sync.dma_start(out=x_w[:].bitcast(I32), in_=words_of(x_words))
-        load_scales([nc.sync] * 4, w1_s, w1_scales)
+        load_scales([nc.sync] * PACK, w1_s, w1_scales)
         nc.sync.dma_start(out=w2_w[:].bitcast(I32), in_=words_of(w2_words))
-        nc.sync.dma_start(out=g_sb[0][:], in_=g_rows[:, 0, :])
-        load_scales([nc.sync] * 4, w2_s, w2_scales)
-        nc.sync.dma_start(out=g_sb[1][:], in_=g_rows[:, 1, :])
+        for t in (0, 1):
+            nc.sync.dma_start(out=g_sb[t][:], in_=g_rows[:, t, :])
+        load_scales([nc.sync] * PACK, w2_s, w2_scales)
         for t in (0, 1):
             nc.sync.dma_start(out=b_sb[t][:], in_=b_rows[:, t, :])
         for t in (2, 3):
@@ -75,16 +79,17 @@ def tile_picked_adain8_gelu_po_kernel(
             nc.sync.dma_start(out=b_sb[t][:], in_=b_rows[:, t, :])
 
         warm = keep.tile([P, 2], F32, name="warm")
-        nc.gpsimd.memset(warm[:, 0:1], 1.0)
+        nc.vector.memset(warm[:, 0:1], 1.0)
         nc.scalar.activation(warm[:, 1:2], warm[:, 0:1], ACT.Abs_reciprocal_sqrt, bias=EPS)
 
         xg_w = keep.tile([P, S], U32, name="xg_w", align_bytes=64)
         xg_s = keep.tile([P, S], U8, name="xg_s", align_bytes=64)
-
         w1_d = keep.tile([P, H], U32, name="w1_d", align_bytes=64)
 
         def deal(dst, src):
-            nc.vector.tensor_copy(out=dst[:].rearrange("p (t m) -> p m t", t=PACK), in_=src[:].rearrange("p (m t) -> p m t", t=PACK))
+            nc.vector.tensor_copy(
+                out=dst[:].rearrange("p (t m) -> p m t", t=PACK), in_=src[:].rearrange("p (m t) -> p m t", t=PACK)
+            )
 
         nc.vector.tensor_copy(xg_s[:], x_s[:].indirect(offs_sb[:]))
         deal(w1_d, w1_w)
@@ -142,7 +147,7 @@ def tile_picked_adain8_gelu_po_kernel(
 
         def modulate(pair, first, width, product_tag, sum_tag):
             cols = slice(first, first + width)
-            lists = sty_sb[:, first // 16 : (first + width) // 16]
+            lists = sty_sb[:, first // GROUP : (first + width) // GROUP]
             scaled = keep.tile([P, 2, width], F32, name="scaled%d_%d" % (pair, first), tag=product_tag, align_bytes=64)
             for e in range(2):
                 t = 2 * pair + e
@@ -162,35 +167,35 @@ def tile_picked_adain8_gelu_po_kernel(
             z_w = keep.tile([P, CHUNK], U32, name="z_w%d" % c, align_bytes=64)
             z_s = keep.tile([P, CHUNK], U8, name="z_s%d" % c, align_bytes=64)
             nc.vector.quantize_mx(out=z_w[:].bitcast(FP8X4), scales=z_s[:], in_=z_sb[c][:].rearrange("p j t -> p (j t)"))
-            if c < 3:
+            if c < LAST_CHUNK:
                 acc = psum.tile([P, PACK, CHUNK], F32, name="acc%d" % c)
-                banks = [acc[:, 0:2, :], acc[:, 2:4, :]]
+                banks = [acc[:]]
             else:
                 low = psum.tile([P, 2, CHUNK], F32, name="acc3_low")
                 high = psum.tile([P, 2, CHUNK], F32, name="acc3_high", tag="y0")
-                acc = None
                 banks = [low[:], high[:]]
+            per_bank = PACK // len(banks)
             for t in range(PACK):
                 wc = slice(t * P, (t + 1) * P)
                 nc.tensor.matmul_mx(
-                    out=banks[t // 2][:, t % 2, :], lhsT=w2_d[:, wc].bitcast(FP8X4), lhsT_scale=w2s_d[:, wc],
+                    out=banks[t // per_bank][:, t % per_bank, :], lhsT=w2_d[:, wc].bitcast(FP8X4), lhsT_scale=w2s_d[:, wc],
                     rhs=z_w[:].bitcast(FP8X4), rhs_scale=z_s[:], start=True, stop=True,
                 )
-            return acc, banks
+            return banks
 
-        def hand_out(c, acc, banks, o_w):
+        def hand_out(c, banks, codes):
             ccols = slice(c * CHUNK, (c + 1) * CHUNK)
             o32 = keep.tile([P, PACK, CHUNK], F32, name="o32_%d" % c)
             o16 = keep.tile([P, CHUNK, PACK], BF16, name="o16_%d" % c, align_bytes=64)
-            if c < 3:
-                nc.scalar.copy(o32[:], acc[:])
+            if c < LAST_CHUNK:
+                nc.scalar.copy(o32[:], banks[0])
             else:
                 nc.scalar.copy(o32[:, 0:2, :], banks[0])
                 nc.vector.tensor_copy(o32[:, 2:4, :], banks[1])
             nc.sync.dma_start(out=out_rows[:, :, ccols], in_=o32[:])
             nc.vector.tensor_copy(o16[:], o32[:].rearrange("p t j -> p j t"))
             nc.vector.quantize_mx(
-                out=o_w[:, (c % 2) * CHUNK : (c % 2 + 1) * CHUNK].bitcast(FP8X4), scales=o_s[:, ccols],
+                out=codes[:, (c % 2) * CHUNK : (c % 2 + 1) * CHUNK].bitcast(FP8X4), scales=o_s[:, ccols],
                 in_=o16[:].rearrange("p j t -> p (j t)"),
             )
 
@@ -199,14 +204,15 @@ def tile_picked_adain8_gelu_po_kernel(
         modulate(0, 0, S, "scaled0", "u_low")
         modulate(1, 0, HALF, "scaled1", "u_first")
         products = [second_product(0), second_product(1)]
-        hand_out(0, *products[0], o_w[0])
-        modulate(1, HALF, HALF, "scaled1", "z1")
+        hand_out(0, products[0], o_w[0])
+        modulate(1, HALF, HALF, "scaled1", "z0")
         products = products + [second_product(2), second_product(3)]
-        hand_out(1, *products[1], o_w[0])
+        hand_out(1, products[1], o_w[0])
         nc.sync.dma_start(out=out_words[:, 0:HALF], in_=o_w[0][:].bitcast(I32))
         for c in (2, 3):
-            hand_out(c, *products[c], o_w[1])
+            hand_out(c, products[c], o_w[1])
+
         nc.scalar.dma_start(out=out_words[:, HALF:S], in_=o_w[1][:].bitcast(I32))
-        for q in range(4):
-            eng = nc.scalar if q % 2 else nc.sync
-            eng.dma_start(out=out_2[0, 4 * q : 4 * q + 4, :].bitcast(I32), in_=o_s[32 * q : 32 * q + 4, :].bitcast(I32))
+        for r in range(PACK):
+            eng = nc.scalar if r % 2 else nc.sync
+            eng.dma_start(out=out_2[0, r:SCALE_ROWS:PACK, :].bitcast(I32), in_=o_s[r:P:QUADRANT, :].bitcast(I32))

@@ -22,7 +22,6 @@ QUADRANT = 32
 SCALE_ROWS = 16
 HALF = 256
 CHUNK = 128
-LAST_CHUNK = S // CHUNK - 1
 EPS = 1e-5
 
 
@@ -42,10 +41,10 @@ def tile_picked_adain8_gelu_po_kernel(
         sty_sb = keep.tile([P, S // GROUP], U16, name="sty_sb")
         x_w = keep.tile([P, T], U32, name="x_w", tag="x_w", align_bytes=64)
         x_s = keep.tile([P, T], U8, name="x_s", align_bytes=64)
+        w2_s = keep.tile([P, N], U8, name="w2_s", align_bytes=64)
         w1_w = keep.tile([P, H], U32, name="w1_w", align_bytes=64)
         w2_w = keep.tile([P, N], U32, name="w2_w", align_bytes=64)
         w1_s = keep.tile([P, H], U8, name="w1_s", tag="w1_s", align_bytes=64)
-        w2_s = keep.tile([P, N], U8, name="w2_s", align_bytes=64)
         g_sb = [keep.tile([P, U], F32, name="g_sb%d" % t) for t in range(PACK)]
         b_sb = [keep.tile([P, U], F32, name="b_sb%d" % t) for t in range(PACK)]
 
@@ -62,15 +61,15 @@ def tile_picked_adain8_gelu_po_kernel(
                 )
 
         nc.sync.dma_start(offs_sb[:], offs)
-        load_scales([nc.sync, nc.scalar, nc.sync, nc.scalar], x_s, x_scales)
-        nc.sync.dma_start(sty_sb[:], sty)
         nc.sync.dma_start(out=w1_w[:].bitcast(I32), in_=words_of(w1_words))
+        load_scales([nc.scalar, nc.scalar, nc.sync, nc.sync], x_s, x_scales)
         nc.sync.dma_start(out=x_w[:].bitcast(I32), in_=words_of(x_words))
         load_scales([nc.sync] * PACK, w1_s, w1_scales)
         nc.sync.dma_start(out=w2_w[:].bitcast(I32), in_=words_of(w2_words))
         for t in (0, 1):
             nc.sync.dma_start(out=g_sb[t][:], in_=g_rows[:, t, :])
         load_scales([nc.sync] * PACK, w2_s, w2_scales)
+        nc.sync.dma_start(sty_sb[:], sty)
         for t in (0, 1):
             nc.sync.dma_start(out=b_sb[t][:], in_=b_rows[:, t, :])
         for t in (2, 3):
@@ -78,11 +77,6 @@ def tile_picked_adain8_gelu_po_kernel(
         for t in (2, 3):
             nc.sync.dma_start(out=b_sb[t][:], in_=b_rows[:, t, :])
 
-        warm = keep.tile([P, 2], F32, name="warm")
-        nc.vector.memset(warm[:, 0:1], 1.0)
-        nc.scalar.activation(warm[:, 1:2], warm[:, 0:1], ACT.Abs_reciprocal_sqrt, bias=EPS)
-
-        xg_w = keep.tile([P, S], U32, name="xg_w", align_bytes=64)
         xg_s = keep.tile([P, S], U8, name="xg_s", align_bytes=64)
         w1_d = keep.tile([P, H], U32, name="w1_d", align_bytes=64)
 
@@ -91,71 +85,107 @@ def tile_picked_adain8_gelu_po_kernel(
                 out=dst[:].rearrange("p (t m) -> p m t", t=PACK), in_=src[:].rearrange("p (m t) -> p m t", t=PACK)
             )
 
-        nc.vector.tensor_copy(xg_s[:], x_s[:].indirect(offs_sb[:]))
-        deal(w1_d, w1_w)
-        nc.vector.tensor_copy(xg_w[:], x_w[:].indirect(offs_sb[:]))
-        w1s_d = keep.tile([P, H], U8, name="w1s_d", tag="x_w", align_bytes=64)
-        deal(w1s_d, w1_s)
-        w2_d = keep.tile([P, N], U32, name="w2_d", tag="w1_s", align_bytes=64)
-        deal(w2_d, w2_w)
-
-        y_ps, moments, rstd, neg_mean, shift, h_sb = [], [], [], [], [], []
-
-        def first_product(t):
-            cols = slice(t * P, (t + 1) * P)
-            y = psum.tile([P, S], F32, name="y%d" % t, tag="y%d" % t)
-            nc.tensor.matmul_mx(
-                out=y[:], lhsT=w1_d[:, cols].bitcast(FP8X4), lhsT_scale=w1s_d[:, cols],
-                rhs=xg_w[:].bitcast(FP8X4), rhs_scale=xg_s[:], start=True, stop=True,
+        def deal_bytes(dst, src):
+            nc.gpsimd.tensor_copy(
+                out=dst[:].rearrange("p (t m) -> p t m", t=PACK), in_=src[:].rearrange("p (m t) -> p t m", t=PACK)
             )
-            stats = keep.tile([P, 6], F32, name="stats%d" % t, tag="stats%d" % t, align_bytes=64)
-            mv = keep.tile([P, 2], F32, name="mv%d" % t, tag="mv%d" % t)
-            nc.vector.bn_stats(stats[:], y[:])
-            nc.vector.bn_aggr(mv[:], stats[:])
-            y_ps.append(y)
-            moments.append(mv)
 
-        def scale_of(t):
-            rstd.append(keep.tile([P, 1], F32, name="rstd%d" % t))
-            neg_mean.append(keep.tile([P, 1], F32, name="neg_mean%d" % t))
-            nc.scalar.activation(rstd[t][:], moments[t][:, 1:2], ACT.Abs_reciprocal_sqrt, bias=EPS)
-            nc.scalar.activation(neg_mean[t][:], moments[t][:, 0:1], ACT.Identity, scale=-1.0)
+        halves = [slice(0, HALF), slice(HALF, S)]
+        half_lists = [slice(0, HALF // GROUP), slice(HALF // GROUP, S // GROUP)]
 
-        def shift_of(t):
-            shift.append(keep.tile([P, 1], F32, name="shift%d" % t))
-            nc.scalar.activation(shift[t][:], neg_mean[t][:], ACT.Identity, scale=rstd[t][:])
+        deal(w1_d, w1_w)
+        nc.vector.tensor_copy(xg_s[:], x_s[:].indirect(offs_sb[:]))
+        xg_w = [keep.tile([P, HALF], U32, name="xg_w%d" % a, align_bytes=64) for a in range(2)]
+        for a in range(2):
+            nc.vector.tensor_copy(xg_w[a][:], x_w[:].indirect(offs_sb[:, half_lists[a]]))
+        w1s_d = keep.tile([P, H], U8, name="w1s_d", align_bytes=64)
+        deal_bytes(w1s_d, w1_s)
 
-        def normalise(t):
-            h_sb.append(keep.tile([P, S], F32, name="h%d" % t, tag="mv%d" % (t + 1)))
-            nc.scalar.activation(h_sb[t][:], y_ps[t][:], ACT.Identity, bias=shift[t][:], scale=rstd[t][:])
+        def first_product(out, t, a):
+            wc = slice(t * P, (t + 1) * P)
+            nc.tensor.matmul_mx(
+                out=out, lhsT=w1_d[:, wc].bitcast(FP8X4), lhsT_scale=w1s_d[:, wc],
+                rhs=xg_w[a][:].bitcast(FP8X4), rhs_scale=xg_s[:, halves[a]], start=True, stop=True,
+            )
 
-        for t in range(PACK):
-            first_product(t)
-        w2s_d = keep.tile([P, N], U8, name="w2s_d", tag="stats3", align_bytes=64)
-        deal(w2s_d, w2_s)
-        scale_of(0)
-        for t in range(PACK):
-            shift_of(t)
-            if t + 1 < PACK:
-                scale_of(t + 1)
-            normalise(t)
+        y0 = [psum.tile([P, HALF], F32, name="y0_%d" % a, tag="y0_%d" % a) for a in range(2)]
+        y_ps = [None] + [psum.tile([P, S], F32, name="y%d" % t, tag="y%d" % t) for t in range(1, PACK)]
+        first_product(y0[0][:], 0, 0)
+        first_product(y_ps[1][:, halves[0]], 1, 0)
+        first_product(y0[1][:], 0, 1)
+        first_product(y_ps[1][:, halves[1]], 1, 1)
+        for t in (2, 3):
+            for a in range(2):
+                first_product(y_ps[t][:, halves[a]], t, a)
+
+        stats0 = keep.tile([P, 2, 6], F32, name="stats0", tag="stats0", align_bytes=64)
+        w2_d = keep.tile([P, N], U32, name="w2_d", tag="x_w", align_bytes=64)
+        deal(w2_d, w2_w)
+        nc.vector.bn_stats(stats0[:, 0, :], y0[0][:])
+        nc.vector.bn_stats(stats0[:, 1, :], y0[1][:])
+        moments = [keep.tile([P, 2], F32, name="mv%d" % t, tag="mv%d" % t, align_bytes=64) for t in range(PACK)]
+        nc.vector.bn_aggr(moments[0][:], stats0[:].rearrange("p a s -> p (a s)"))
+        stats = keep.tile([P, 3, 6], F32, name="stats", tag="stats0", align_bytes=64)
+        for t in range(1, PACK + 1):
+            if t < PACK:
+                nc.vector.bn_stats(stats[:, t - 1, :], y_ps[t][:])
+            if t > 1:
+                nc.vector.bn_aggr(moments[t - 1][:], stats[:, t - 2, :])
+        w2s_d = keep.tile([P, N], U8, name="w2s_d", tag="mv0", align_bytes=64)
+        deal_bytes(w2s_d, w2_s)
+
+        h_sb = [keep.tile([P, S], F32, name="h%d" % t) for t in range(PACK)]
+
+        def column(name, tag):
+            return keep.tile([P, 1], F32, name=name, tag=tag, align_bytes=64)
+
+        def scale_of(t, tag):
+            both = keep.tile([P, 2], F32, name="rstd_neg_mean%d" % t, tag=tag, align_bytes=64)
+            nc.scalar.activation(both[:, 0:1], moments[t][:, 1:2], ACT.Abs_reciprocal_sqrt, bias=EPS)
+            nc.scalar.activation(both[:, 1:2], moments[t][:, 0:1], ACT.Identity, scale=-1.0)
+            return both[:, 0:1], both[:, 1:2]
+
+        def shift_of(t, rstd, neg_mean):
+            shift = column("shift%d" % t, "shift%d" % t)
+            nc.scalar.activation(shift[:], neg_mean, ACT.Identity, scale=rstd)
+            return shift[:]
+
+        def normalise(out, y, rstd, shift):
+            nc.scalar.activation(out, y, ACT.Identity, bias=shift, scale=rstd)
+
+        rstd0 = column("rstd0", "rstd0")[:]
+        neg_mean0 = column("neg_mean0", "neg_mean0")[:]
+        nc.scalar.activation(rstd0, moments[0][:, 1:2], ACT.Abs_reciprocal_sqrt, bias=EPS)
+        nc.scalar.activation(neg_mean0, moments[0][:, 0:1], ACT.Identity, scale=-1.0)
+        shift0 = shift_of(0, rstd0, neg_mean0)
+        for a in range(2):
+            normalise(h_sb[0][:, halves[a]], y0[a][:], rstd0, shift0)
+        for t in range(1, PACK):
+            rstd, neg_mean = scale_of(t, "neg_mean0" if t < 3 else "shift1")
+            normalise(h_sb[t][:], y_ps[t][:], rstd, shift_of(t, rstd, neg_mean))
 
         out_rows = out_0.rearrange("(p t) j -> p t j", t=PACK)
         out_words = out_1[0].rearrange("p n t -> p (n t)").bitcast(I32)
         o_s = keep.tile([P, S], U8, name="o_s", align_bytes=64)
-        z_sb = [keep.tile([P, CHUNK, PACK], BF16, name="z%d" % c, tag="z%d" % c, align_bytes=64) for c in range(S // CHUNK)]
+        z_first = [keep.tile([P, CHUNK, PACK], BF16, name="z%d" % c, tag=tag, align_bytes=64) for c, tag in enumerate(["z0", "z1"])]
+        z_second = keep.tile([P, 2, CHUNK, PACK], BF16, name="z_second", align_bytes=64)
+        z_sb = [z_first[0][:], z_first[1][:], z_second[:, 0, :, :], z_second[:, 1, :, :]]
 
-        def modulate(pair, first, width, product_tag, sum_tag):
-            cols = slice(first, first + width)
+        def look_up(out, table, first, width, other, op):
             lists = sty_sb[:, first // GROUP : (first + width) // GROUP]
-            scaled = keep.tile([P, 2, width], F32, name="scaled%d_%d" % (pair, first), tag=product_tag, align_bytes=64)
+            nc.vector.tensor_tensor(out, table[:].indirect(lists), other, op)
+
+        def products(pair, first, width, tag):
+            scaled = keep.tile([P, 2, width], F32, name="scaled%d_%d" % (pair, first), tag=tag, align_bytes=64)
             for e in range(2):
                 t = 2 * pair + e
-                nc.vector.tensor_tensor(scaled[:, e, :], g_sb[t][:].indirect(lists), h_sb[t][:, cols], ALU.mult)
-            u = keep.tile([P, 2, width], F32, name="u%d_%d" % (pair, first), tag=sum_tag, align_bytes=64)
+                look_up(scaled[:, e, :], g_sb[t], first, width, h_sb[t][:, first : first + width], ALU.mult)
+            return scaled
+
+        def sums(pair, first, width, scaled, tag):
+            u = keep.tile([P, 2, width], F32, name="u%d_%d" % (pair, first), tag=tag, align_bytes=64)
             for e in range(2):
-                t = 2 * pair + e
-                nc.vector.tensor_tensor(u[:, e, :], b_sb[t][:].indirect(lists), scaled[:, e, :], ALU.add)
+                look_up(u[:, e, :], b_sb[2 * pair + e], first, width, scaled[:, e, :], ALU.add)
             for cc in range(width // CHUNK):
                 nc.scalar.activation(
                     z_sb[first // CHUNK + cc][:, :, 2 * pair : 2 * pair + 2],
@@ -163,18 +193,12 @@ def tile_picked_adain8_gelu_po_kernel(
                     ACT.Gelu_apprx_tanh,
                 )
 
-        def second_product(c):
+        def second_product(c, bank_tags):
             z_w = keep.tile([P, CHUNK], U32, name="z_w%d" % c, align_bytes=64)
             z_s = keep.tile([P, CHUNK], U8, name="z_s%d" % c, align_bytes=64)
-            nc.vector.quantize_mx(out=z_w[:].bitcast(FP8X4), scales=z_s[:], in_=z_sb[c][:].rearrange("p j t -> p (j t)"))
-            if c < LAST_CHUNK:
-                acc = psum.tile([P, PACK, CHUNK], F32, name="acc%d" % c)
-                banks = [acc[:]]
-            else:
-                low = psum.tile([P, 2, CHUNK], F32, name="acc3_low")
-                high = psum.tile([P, 2, CHUNK], F32, name="acc3_high", tag="y0")
-                banks = [low[:], high[:]]
-            per_bank = PACK // len(banks)
+            nc.vector.quantize_mx(out=z_w[:].bitcast(FP8X4), scales=z_s[:], in_=z_sb[c].rearrange("p j t -> p (j t)"))
+            per_bank = PACK // len(bank_tags)
+            banks = [psum.tile([P, per_bank, CHUNK], F32, name="acc%d_%s" % (c, tag), tag=tag) for tag in bank_tags]
             for t in range(PACK):
                 wc = slice(t * P, (t + 1) * P)
                 nc.tensor.matmul_mx(
@@ -183,36 +207,51 @@ def tile_picked_adain8_gelu_po_kernel(
                 )
             return banks
 
-        def hand_out(c, banks, codes):
-            ccols = slice(c * CHUNK, (c + 1) * CHUNK)
-            o32 = keep.tile([P, PACK, CHUNK], F32, name="o32_%d" % c)
-            o16 = keep.tile([P, CHUNK, PACK], BF16, name="o16_%d" % c, align_bytes=64)
-            if c < LAST_CHUNK:
-                nc.scalar.copy(o32[:], banks[0])
-            else:
-                nc.scalar.copy(o32[:, 0:2, :], banks[0])
-                nc.vector.tensor_copy(o32[:, 2:4, :], banks[1])
-            nc.sync.dma_start(out=out_rows[:, :, ccols], in_=o32[:])
-            nc.vector.tensor_copy(o16[:], o32[:].rearrange("p t j -> p j t"))
+        o32 = [keep.tile([P, PACK, CHUNK], F32, name="o32_%d" % c) for c in range(S // CHUNK)]
+        o16 = [keep.tile([P, 2, CHUNK, PACK], BF16, name="o16_%d" % a, align_bytes=64) for a in range(2)]
+        o_w = [keep.tile([P, HALF], U32, name="o_w%d" % a, align_bytes=64) for a in range(2)]
+
+        def store(c):
+            nc.sync.dma_start(out=out_rows[:, :, c * CHUNK : (c + 1) * CHUNK], in_=o32[c][:])
+
+        def round_out(c):
+            nc.vector.tensor_copy(o16[c // 2][:, c % 2, :, :], o32[c][:].rearrange("p t j -> p j t"))
+
+        def quantise_out(a, first, count):
+            cols = slice(first * CHUNK, (first + count) * CHUNK)
             nc.vector.quantize_mx(
-                out=codes[:, (c % 2) * CHUNK : (c % 2 + 1) * CHUNK].bitcast(FP8X4), scales=o_s[:, ccols],
-                in_=o16[:].rearrange("p j t -> p (j t)"),
+                out=o_w[a][:, cols].bitcast(FP8X4), scales=o_s[:, a * HALF + first * CHUNK : a * HALF + (first + count) * CHUNK],
+                in_=o16[a][:, first : first + count, :, :].rearrange("p c j t -> p (c j t)"),
             )
 
-        o_w = [keep.tile([P, HALF], U32, name="o_w%d" % half, align_bytes=64) for half in range(2)]
+        sums(0, 0, S, products(0, 0, S, "scaled0"), "u_low")
+        sums(1, 0, HALF, products(1, 0, HALF, "scaled1"), "u_first")
+        scaled = products(1, HALF, HALF, "scaled1")
+        acc0 = second_product(0, ["acc0"])
+        acc1 = second_product(1, ["acc1"])
+        nc.scalar.copy(o32[0][:], acc0[0][:])
+        store(0)
+        sums(1, HALF, HALF, scaled, "z0")
+        round_out(0)
+        acc2 = second_product(2, ["acc2"])
+        quantise_out(0, 0, 1)
+        acc3 = second_product(3, ["y0_0", "y0_1"])
+        nc.scalar.copy(o32[1][:], acc1[0][:])
+        store(1)
+        round_out(1)
+        quantise_out(0, 1, 1)
+        nc.sync.dma_start(out=out_words[:, halves[0]], in_=o_w[0][:].bitcast(I32))
+        nc.scalar.copy(o32[2][:], acc2[0][:])
+        store(2)
+        nc.scalar.copy(o32[3][:, 0:2, :], acc3[0][:])
+        nc.vector.tensor_copy(o32[3][:, 2:4, :], acc3[1][:])
+        store(3)
+        round_out(2)
+        round_out(3)
+        quantise_out(1, 0, 1)
+        quantise_out(1, 1, 1)
 
-        modulate(0, 0, S, "scaled0", "u_low")
-        modulate(1, 0, HALF, "scaled1", "u_first")
-        products = [second_product(0), second_product(1)]
-        hand_out(0, products[0], o_w[0])
-        modulate(1, HALF, HALF, "scaled1", "z0")
-        products = products + [second_product(2), second_product(3)]
-        hand_out(1, products[1], o_w[0])
-        nc.sync.dma_start(out=out_words[:, 0:HALF], in_=o_w[0][:].bitcast(I32))
-        for c in (2, 3):
-            hand_out(c, products[c], o_w[1])
-
-        nc.scalar.dma_start(out=out_words[:, HALF:S], in_=o_w[1][:].bitcast(I32))
+        nc.scalar.dma_start(out=out_words[:, halves[1]], in_=o_w[1][:].bitcast(I32))
         for r in range(PACK):
             eng = nc.scalar if r % 2 else nc.sync
             eng.dma_start(out=out_2[0, r:SCALE_ROWS:PACK, :].bitcast(I32), in_=o_s[r:P:QUADRANT, :].bitcast(I32))

@@ -110,11 +110,9 @@ def tile_picked_adain8_gelu_po_kernel(
 
         y0 = [psum.tile([P, HALF], F32, name="y0_%d" % a, tag="y0_%d" % a) for a in range(2)]
         y_ps = [None] + [psum.tile([P, S], F32, name="y%d" % t, tag="y%d" % t) for t in range(1, PACK)]
-        first_product(y0[0][:], 0, 0)
-        first_product(y_ps[1][:, halves[0]], 1, 0)
-        first_product(y0[1][:], 0, 1)
-        first_product(y_ps[1][:, halves[1]], 1, 1)
-        for t in (2, 3):
+        for a in range(2):
+            first_product(y0[a][:], 0, a)
+        for t in range(1, PACK):
             for a in range(2):
                 first_product(y_ps[t][:, halves[a]], t, a)
 
@@ -123,14 +121,13 @@ def tile_picked_adain8_gelu_po_kernel(
         deal(w2_d, w2_w)
         nc.vector.bn_stats(stats0[:, 0, :], y0[0][:])
         nc.vector.bn_stats(stats0[:, 1, :], y0[1][:])
-        moments = [keep.tile([P, 2], F32, name="mv%d" % t, tag="mv%d" % t, align_bytes=64) for t in range(PACK)]
+        moments = [keep.tile([P, 2], F32, name="mv%d" % t, tag="mv%d" % t, align_bytes=64) for t in range(3)]
         nc.vector.bn_aggr(moments[0][:], stats0[:].rearrange("p a s -> p (a s)"))
-        stats = keep.tile([P, 3, 6], F32, name="stats", tag="stats0", align_bytes=64)
-        for t in range(1, PACK + 1):
-            if t < PACK:
-                nc.vector.bn_stats(stats[:, t - 1, :], y_ps[t][:])
-            if t > 1:
-                nc.vector.bn_aggr(moments[t - 1][:], stats[:, t - 2, :])
+        stats = keep.tile([P, 2, 6], F32, name="stats", tag="stats0", align_bytes=64)
+        for t in (1, 2):
+            nc.vector.bn_stats(stats[:, t - 1, :], y_ps[t][:])
+        for t in (1, 2):
+            nc.vector.bn_aggr(moments[t][:], stats[:, t - 1, :])
         w2s_d = keep.tile([P, N], U8, name="w2s_d", tag="mv0", align_bytes=64)
         deal_bytes(w2s_d, w2_s)
 
@@ -160,16 +157,29 @@ def tile_picked_adain8_gelu_po_kernel(
         shift0 = shift_of(0, rstd0, neg_mean0)
         for a in range(2):
             normalise(h_sb[0][:, halves[a]], y0[a][:], rstd0, shift0)
-        for t in range(1, PACK):
-            rstd, neg_mean = scale_of(t, "neg_mean0" if t < 3 else "shift1")
-            normalise(h_sb[t][:], y_ps[t][:], rstd, shift_of(t, rstd, neg_mean))
+        rstd1, neg_mean1 = scale_of(1, "neg_mean0")
+        normalise(h_sb[1][:], y_ps[1][:], rstd1, shift_of(1, rstd1, neg_mean1))
+        rstd2, neg_mean2 = scale_of(2, "neg_mean0")
+        sum3 = column("sum3", "sum3")
+        y3_sb = keep.tile([P, S], F32, name="y3_sb", tag="shift1", align_bytes=64)
+        nc.scalar.activation(y3_sb[:], y_ps[3][:], ACT.Copy, accum_out=sum3[:])
+        shift2 = shift_of(2, rstd2, neg_mean2)
+        neg_mean3 = column("neg_mean3", "neg_mean3")
+        nc.scalar.activation(neg_mean3[:], sum3[:], ACT.Identity, scale=-1.0 / S)
+        squares3 = keep.tile([P, S], BF16, name="squares3")
+        sum_squares3 = column("sum_squares3", "sum_squares3")
+        nc.scalar.activation(squares3[:], y3_sb[:], ACT.Square, bias=neg_mean3[:], accum_out=sum_squares3[:])
+        normalise(h_sb[2][:], y_ps[2][:], rstd2, shift2)
+        rstd3 = column("rstd3", "rstd3")
+        nc.scalar.activation(rstd3[:], sum_squares3[:], ACT.Abs_reciprocal_sqrt, bias=EPS, scale=1.0 / S)
+        shift3 = shift_of(3, rstd3[:], neg_mean3[:])
+        normalise(h_sb[3][:], y3_sb[:], rstd3[:], shift3)
 
         out_rows = out_0.rearrange("(p t) j -> p t j", t=PACK)
         out_words = out_1[0].rearrange("p n t -> p (n t)").bitcast(I32)
         o_s = keep.tile([P, S], U8, name="o_s", align_bytes=64)
-        z_first = [keep.tile([P, CHUNK, PACK], BF16, name="z%d" % c, tag=tag, align_bytes=64) for c, tag in enumerate(["z0", "z1"])]
-        z_second = keep.tile([P, 2, CHUNK, PACK], BF16, name="z_second", align_bytes=64)
-        z_sb = [z_first[0][:], z_first[1][:], z_second[:, 0, :, :], z_second[:, 1, :, :]]
+        z_first = [keep.tile([P, CHUNK, PACK], BF16, name="z%d" % c, tag=tag, align_bytes=64) for c, tag in enumerate(["shift3", "rstd3"])]
+        z_sb = [z_first[0][:], z_first[1][:]]
 
         def look_up(out, table, first, width, other, op):
             lists = sty_sb[:, first // GROUP : (first + width) // GROUP]
@@ -186,12 +196,11 @@ def tile_picked_adain8_gelu_po_kernel(
             u = keep.tile([P, 2, width], F32, name="u%d_%d" % (pair, first), tag=tag, align_bytes=64)
             for e in range(2):
                 look_up(u[:, e, :], b_sb[2 * pair + e], first, width, scaled[:, e, :], ALU.add)
-            for cc in range(width // CHUNK):
-                nc.scalar.activation(
-                    z_sb[first // CHUNK + cc][:, :, 2 * pair : 2 * pair + 2],
-                    u[:, :, cc * CHUNK : (cc + 1) * CHUNK].rearrange("p e j -> p j e"),
-                    ACT.Gelu_apprx_tanh,
-                )
+            return u
+
+        def gelu(pair, c, u, first):
+            cols = slice(c * CHUNK - first, (c + 1) * CHUNK - first)
+            nc.scalar.activation(z_sb[c][:, :, 2 * pair : 2 * pair + 2], u[:, :, cols].rearrange("p e j -> p j e"), ACT.Gelu_apprx_tanh)
 
         def second_product(c, bank_tags):
             z_w = keep.tile([P, CHUNK], U32, name="z_w%d" % c, align_bytes=64)
@@ -224,14 +233,24 @@ def tile_picked_adain8_gelu_po_kernel(
                 in_=o16[a][:, first : first + count, :, :].rearrange("p c j t -> p (c j t)"),
             )
 
-        sums(0, 0, S, products(0, 0, S, "scaled0"), "u_low")
-        sums(1, 0, HALF, products(1, 0, HALF, "scaled1"), "u_first")
+        u_low = sums(0, 0, S, products(0, 0, S, "scaled0"), "u_low")
+        for c in (0, 1):
+            gelu(0, c, u_low, 0)
+        u_first = sums(1, 0, HALF, products(1, 0, HALF, "scaled1"), "u_first")
+        for c in (0, 1):
+            gelu(1, c, u_first, 0)
+        z_second = keep.tile([P, 2, CHUNK, PACK], BF16, name="z_second", tag="u_first", align_bytes=64)
+        z_sb.extend([z_second[:, 0, :, :], z_second[:, 1, :, :]])
+        for c in (2, 3):
+            gelu(0, c, u_low, 0)
         scaled = products(1, HALF, HALF, "scaled1")
         acc0 = second_product(0, ["acc0"])
         acc1 = second_product(1, ["acc1"])
         nc.scalar.copy(o32[0][:], acc0[0][:])
         store(0)
-        sums(1, HALF, HALF, scaled, "z0")
+        u_second = sums(1, HALF, HALF, scaled, "shift3")
+        for c in (2, 3):
+            gelu(1, c, u_second, HALF)
         round_out(0)
         acc2 = second_product(2, ["acc2"])
         quantise_out(0, 0, 1)

@@ -66,10 +66,10 @@ def tile_picked_adain8_gelu_po_kernel(
         nc.sync.dma_start(out=x_w[:].bitcast(I32), in_=words_of(x_words))
         load_scales([nc.sync] * PACK, w1_s, w1_scales)
         nc.sync.dma_start(out=w2_w[:].bitcast(I32), in_=words_of(w2_words))
-        for t in (0, 1):
-            nc.sync.dma_start(out=g_sb[t][:], in_=g_rows[:, t, :])
-        load_scales([nc.sync] * PACK, w2_s, w2_scales)
         nc.sync.dma_start(sty_sb[:], sty)
+        nc.sync.dma_start(out=g_sb[0][:], in_=g_rows[:, 0, :])
+        load_scales([nc.sync] * PACK, w2_s, w2_scales)
+        nc.sync.dma_start(out=g_sb[1][:], in_=g_rows[:, 1, :])
         for t in (0, 1):
             nc.sync.dma_start(out=b_sb[t][:], in_=b_rows[:, t, :])
         for t in (2, 3):
@@ -108,27 +108,35 @@ def tile_picked_adain8_gelu_po_kernel(
                 rhs=xg_w[a][:].bitcast(FP8X4), rhs_scale=xg_s[:, halves[a]], start=True, stop=True,
             )
 
-        y0 = [psum.tile([P, HALF], F32, name="y0_%d" % a, tag="y0_%d" % a) for a in range(2)]
-        y_ps = [None] + [psum.tile([P, S], F32, name="y%d" % t, tag="y%d" % t) for t in range(1, PACK)]
-        for a in range(2):
-            first_product(y0[a][:], 0, a)
-        for t in range(1, PACK):
+        y_half = [[psum.tile([P, HALF], F32, name="y%d_%d" % (t, a), tag="y%d_%d" % (t, a)) for a in range(2)] for t in range(3)]
+        y3 = psum.tile([P, S], F32, name="y3", tag="y3")
+        for t in range(3):
             for a in range(2):
-                first_product(y_ps[t][:, halves[a]], t, a)
+                first_product(y_half[t][a][:], t, a)
+        for a in range(2):
+            first_product(y3[:, halves[a]], 3, a)
 
-        stats0 = keep.tile([P, 2, 6], F32, name="stats0", tag="stats0", align_bytes=64)
         w2_d = keep.tile([P, N], U32, name="w2_d", tag="x_w", align_bytes=64)
         deal(w2_d, w2_w)
-        nc.vector.bn_stats(stats0[:, 0, :], y0[0][:])
-        nc.vector.bn_stats(stats0[:, 1, :], y0[1][:])
+        stats = [keep.tile([P, 2, 6], F32, name="stats%d" % t, align_bytes=64) for t in range(3)]
         moments = [keep.tile([P, 2], F32, name="mv%d" % t, tag="mv%d" % t, align_bytes=64) for t in range(3)]
-        nc.vector.bn_aggr(moments[0][:], stats0[:].rearrange("p a s -> p (a s)"))
-        stats = keep.tile([P, 2, 6], F32, name="stats", tag="stats0", align_bytes=64)
-        for t in (1, 2):
-            nc.vector.bn_stats(stats[:, t - 1, :], y_ps[t][:])
-        for t in (1, 2):
-            nc.vector.bn_aggr(moments[t][:], stats[:, t - 1, :])
-        w2s_d = keep.tile([P, N], U8, name="w2s_d", tag="mv0", align_bytes=64)
+
+        def half_stats(t, a):
+            nc.vector.bn_stats(stats[t][:, a, :], y_half[t][a][:])
+
+        def aggregate(t):
+            nc.vector.bn_aggr(moments[t][:], stats[t][:].rearrange("p a s -> p (a s)"))
+
+        half_stats(0, 0)
+        half_stats(0, 1)
+        half_stats(1, 0)
+        aggregate(0)
+        half_stats(1, 1)
+        half_stats(2, 0)
+        aggregate(1)
+        half_stats(2, 1)
+        aggregate(2)
+        w2s_d = keep.tile([P, N], U8, name="w2s_d", align_bytes=64)
         deal_bytes(w2s_d, w2_s)
 
         h_sb = [keep.tile([P, S], F32, name="h%d" % t) for t in range(PACK)]
@@ -150,40 +158,44 @@ def tile_picked_adain8_gelu_po_kernel(
         def normalise(out, y, rstd, shift):
             nc.scalar.activation(out, y, ACT.Identity, bias=shift, scale=rstd)
 
+        def look_up(out, table, first, width, other, op):
+            lists = sty_sb[:, first // GROUP : (first + width) // GROUP]
+            nc.vector.tensor_tensor(out, table[:].indirect(lists), other, op)
+
         rstd0 = column("rstd0", "rstd0")[:]
-        neg_mean0 = column("neg_mean0", "neg_mean0")[:]
         nc.scalar.activation(rstd0, moments[0][:, 1:2], ACT.Abs_reciprocal_sqrt, bias=EPS)
-        nc.scalar.activation(neg_mean0, moments[0][:, 0:1], ACT.Identity, scale=-1.0)
-        shift0 = shift_of(0, rstd0, neg_mean0)
         for a in range(2):
-            normalise(h_sb[0][:, halves[a]], y0[a][:], rstd0, shift0)
-        rstd1, neg_mean1 = scale_of(1, "neg_mean0")
-        normalise(h_sb[1][:], y_ps[1][:], rstd1, shift_of(1, rstd1, neg_mean1))
-        rstd2, neg_mean2 = scale_of(2, "neg_mean0")
-        sum3 = column("sum3", "sum3")
-        y3_sb = keep.tile([P, S], F32, name="y3_sb", tag="shift1", align_bytes=64)
-        nc.scalar.activation(y3_sb[:], y_ps[3][:], ACT.Copy, accum_out=sum3[:])
-        shift2 = shift_of(2, rstd2, neg_mean2)
+            nc.scalar.activation(h_sb[0][:, halves[a]], y_half[0][a][:], ACT.Identity, bias=moments[0][:, 0:1], scale=-1.0)
+        raw0 = keep.tile([P, S], F32, name="raw0")
+        look_up(raw0[:], g_sb[0], 0, S, h_sb[0][:], ALU.mult)
+        rstd1, neg_mean1 = scale_of(1, "both1")
+        shift1 = shift_of(1, rstd1, neg_mean1)
+        for a in range(2):
+            normalise(h_sb[1][:, halves[a]], y_half[1][a][:], rstd1, shift1)
+        scaled_low = keep.tile([P, 2, S], F32, name="scaled_low")
+        nc.scalar.activation(scaled_low[:, 0, :], raw0[:], ACT.Identity, scale=rstd0)
+        for a in range(2):
+            look_up(scaled_low[:, 1, halves[a]], g_sb[1], a * HALF, HALF, h_sb[1][:, halves[a]], ALU.mult)
+        rstd2, neg_mean2 = scale_of(2, "both1")
         neg_mean3 = column("neg_mean3", "neg_mean3")
-        nc.scalar.activation(neg_mean3[:], sum3[:], ACT.Identity, scale=-1.0 / S)
+        terms3 = keep.tile([P, S], BF16, name="terms3", tag="shift1", align_bytes=64)
+        nc.scalar.activation(terms3[:], y3[:], ACT.Copy, scale=-1.0 / S, accum_out=neg_mean3[:])
+        shift2 = shift_of(2, rstd2, neg_mean2)
         squares3 = keep.tile([P, S], BF16, name="squares3")
         sum_squares3 = column("sum_squares3", "sum_squares3")
-        nc.scalar.activation(squares3[:], y3_sb[:], ACT.Square, bias=neg_mean3[:], accum_out=sum_squares3[:])
-        normalise(h_sb[2][:], y_ps[2][:], rstd2, shift2)
+        nc.scalar.activation(squares3[:], y3[:], ACT.Square, bias=neg_mean3[:], accum_out=sum_squares3[:])
+        normalise(h_sb[2][:, halves[0]], y_half[2][0][:], rstd2, shift2)
         rstd3 = column("rstd3", "rstd3")
         nc.scalar.activation(rstd3[:], sum_squares3[:], ACT.Abs_reciprocal_sqrt, bias=EPS, scale=1.0 / S)
+        normalise(h_sb[2][:, halves[1]], y_half[2][1][:], rstd2, shift2)
         shift3 = shift_of(3, rstd3[:], neg_mean3[:])
-        normalise(h_sb[3][:], y3_sb[:], rstd3[:], shift3)
+        normalise(h_sb[3][:], y3[:], rstd3[:], shift3)
 
         out_rows = out_0.rearrange("(p t) j -> p t j", t=PACK)
         out_words = out_1[0].rearrange("p n t -> p (n t)").bitcast(I32)
         o_s = keep.tile([P, S], U8, name="o_s", align_bytes=64)
         z_first = [keep.tile([P, CHUNK, PACK], BF16, name="z%d" % c, tag=tag, align_bytes=64) for c, tag in enumerate(["shift3", "rstd3"])]
         z_sb = [z_first[0][:], z_first[1][:]]
-
-        def look_up(out, table, first, width, other, op):
-            lists = sty_sb[:, first // GROUP : (first + width) // GROUP]
-            nc.vector.tensor_tensor(out, table[:].indirect(lists), other, op)
 
         def products(pair, first, width, tag):
             scaled = keep.tile([P, 2, width], F32, name="scaled%d_%d" % (pair, first), tag=tag, align_bytes=64)
@@ -233,7 +245,9 @@ def tile_picked_adain8_gelu_po_kernel(
                 in_=o16[a][:, first : first + count, :, :].rearrange("p c j t -> p (c j t)"),
             )
 
-        u_low = sums(0, 0, S, products(0, 0, S, "scaled0"), "u_low")
+        u_low = keep.tile([P, 2, S], F32, name="u_low", align_bytes=64)
+        look_up(u_low[:, 0, :], b_sb[0], 0, S, scaled_low[:, 0, :], ALU.subtract)
+        look_up(u_low[:, 1, :], b_sb[1], 0, S, scaled_low[:, 1, :], ALU.add)
         for c in (0, 1):
             gelu(0, c, u_low, 0)
         u_first = sums(1, 0, HALF, products(1, 0, HALF, "scaled1"), "u_first")
@@ -244,15 +258,15 @@ def tile_picked_adain8_gelu_po_kernel(
         for c in (2, 3):
             gelu(0, c, u_low, 0)
         scaled = products(1, HALF, HALF, "scaled1")
-        acc0 = second_product(0, ["acc0"])
-        acc1 = second_product(1, ["acc1"])
+        acc0 = second_product(0, ["y1_0"])
+        acc1 = second_product(1, ["y1_1"])
         nc.scalar.copy(o32[0][:], acc0[0][:])
         store(0)
         u_second = sums(1, HALF, HALF, scaled, "shift3")
         for c in (2, 3):
             gelu(1, c, u_second, HALF)
         round_out(0)
-        acc2 = second_product(2, ["acc2"])
+        acc2 = second_product(2, ["y2_0"])
         quantise_out(0, 0, 1)
         acc3 = second_product(3, ["y0_0", "y0_1"])
         nc.scalar.copy(o32[1][:], acc1[0][:])

@@ -45,7 +45,7 @@ def tile_picked_adain8_gelu_po_kernel(
         w1_w = keep.tile([P, H], U32, name="w1_w", align_bytes=64)
         w2_w = keep.tile([P, N], U32, name="w2_w", align_bytes=64)
         w1_s = keep.tile([P, H], U8, name="w1_s", tag="w1_s", align_bytes=64)
-        g_sb = [keep.tile([P, U], F32, name="g_sb%d" % t) for t in range(PACK)]
+        g_sb = [keep.tile([P, U], F32, name="g_sb%d" % t, tag="g_sb%d" % t) for t in range(PACK)]
         b_sb = [keep.tile([P, U], F32, name="b_sb%d" % t) for t in range(PACK)]
 
         for scale_tile in (x_s, w1_s, w2_s):
@@ -118,7 +118,7 @@ def tile_picked_adain8_gelu_po_kernel(
 
         w2_d = keep.tile([P, N], U32, name="w2_d", tag="x_w", align_bytes=64)
         deal(w2_d, w2_w)
-        stats = [keep.tile([P, 2, 6], F32, name="stats%d" % t, align_bytes=64) for t in range(3)]
+        stats = [keep.tile([P, 2, 6], F32, name="stats%d" % t, tag="stats%d" % t, align_bytes=64) for t in range(3)]
         moments = [keep.tile([P, 2], F32, name="mv%d" % t, tag="mv%d" % t, align_bytes=64) for t in range(3)]
 
         def half_stats(t, a):
@@ -139,7 +139,7 @@ def tile_picked_adain8_gelu_po_kernel(
         w2s_d = keep.tile([P, N], U8, name="w2s_d", align_bytes=64)
         deal_bytes(w2s_d, w2_s)
 
-        h_sb = [keep.tile([P, S], F32, name="h%d" % t) for t in range(PACK)]
+        h_sb = [keep.tile([P, S], F32, name="h%d" % t, tag="h%d" % t, align_bytes=64) for t in range(2)]
 
         def column(name, tag):
             return keep.tile([P, 1], F32, name=name, tag=tag, align_bytes=64)
@@ -166,42 +166,47 @@ def tile_picked_adain8_gelu_po_kernel(
         nc.scalar.activation(rstd0, moments[0][:, 1:2], ACT.Abs_reciprocal_sqrt, bias=EPS)
         for a in range(2):
             nc.scalar.activation(h_sb[0][:, halves[a]], y_half[0][a][:], ACT.Identity, bias=moments[0][:, 0:1], scale=-1.0)
-        raw0 = keep.tile([P, S], F32, name="raw0")
+        raw0 = keep.tile([P, S], F32, name="raw0", tag="raw0", align_bytes=64)
         look_up(raw0[:], g_sb[0], 0, S, h_sb[0][:], ALU.mult)
         rstd1, neg_mean1 = scale_of(1, "both1")
+        neg_mean3 = column("neg_mean3", "neg_mean3")
+        terms3 = keep.tile([P, S], BF16, name="terms3", tag="stats1", align_bytes=64)
+        nc.scalar.activation(terms3[:], y3[:], ACT.Copy, scale=-1.0 / S, accum_out=neg_mean3[:])
         shift1 = shift_of(1, rstd1, neg_mean1)
+        rstd2, neg_mean2 = scale_of(2, "both2")
         for a in range(2):
             normalise(h_sb[1][:, halves[a]], y_half[1][a][:], rstd1, shift1)
         scaled_low = keep.tile([P, 2, S], F32, name="scaled_low")
         nc.scalar.activation(scaled_low[:, 0, :], raw0[:], ACT.Identity, scale=rstd0)
         for a in range(2):
             look_up(scaled_low[:, 1, halves[a]], g_sb[1], a * HALF, HALF, h_sb[1][:, halves[a]], ALU.mult)
-        rstd2, neg_mean2 = scale_of(2, "both1")
-        neg_mean3 = column("neg_mean3", "neg_mean3")
-        terms3 = keep.tile([P, S], BF16, name="terms3", tag="shift1", align_bytes=64)
-        nc.scalar.activation(terms3[:], y3[:], ACT.Copy, scale=-1.0 / S, accum_out=neg_mean3[:])
         shift2 = shift_of(2, rstd2, neg_mean2)
-        squares3 = keep.tile([P, S], BF16, name="squares3")
+        h_high = [
+            [keep.tile([P, HALF], F32, name="h%d_%d" % (t, a), tag=tag, align_bytes=64) for a, tag in enumerate(tags)]
+            for t, tags in ((2, ("h0", "raw0")), (3, ("h3_0", "h3_1")))
+        ]
+        squares3 = keep.tile([P, S], BF16, name="squares3", tag="g_sb0")
         sum_squares3 = column("sum_squares3", "sum_squares3")
         nc.scalar.activation(squares3[:], y3[:], ACT.Square, bias=neg_mean3[:], accum_out=sum_squares3[:])
-        normalise(h_sb[2][:, halves[0]], y_half[2][0][:], rstd2, shift2)
+        normalise(h_high[0][0][:], y_half[2][0][:], rstd2, shift2)
         rstd3 = column("rstd3", "rstd3")
         nc.scalar.activation(rstd3[:], sum_squares3[:], ACT.Abs_reciprocal_sqrt, bias=EPS, scale=1.0 / S)
-        normalise(h_sb[2][:, halves[1]], y_half[2][1][:], rstd2, shift2)
+        normalise(h_high[0][1][:], y_half[2][1][:], rstd2, shift2)
         shift3 = shift_of(3, rstd3[:], neg_mean3[:])
-        normalise(h_sb[3][:], y3[:], rstd3[:], shift3)
+        for a in range(2):
+            normalise(h_high[1][a][:], y3[:, halves[a]], rstd3[:], shift3)
 
         out_rows = out_0.rearrange("(p t) j -> p t j", t=PACK)
         out_words = out_1[0].rearrange("p n t -> p (n t)").bitcast(I32)
         o_s = keep.tile([P, S], U8, name="o_s", align_bytes=64)
-        z_first = [keep.tile([P, CHUNK, PACK], BF16, name="z%d" % c, tag=tag, align_bytes=64) for c, tag in enumerate(["shift3", "rstd3"])]
+        z_first = [keep.tile([P, CHUNK, PACK], BF16, name="z%d" % c, tag=tag, align_bytes=64) for c, tag in enumerate(["h3_0", "h0"])]
         z_sb = [z_first[0][:], z_first[1][:]]
 
         def products(pair, first, width, tag):
             scaled = keep.tile([P, 2, width], F32, name="scaled%d_%d" % (pair, first), tag=tag, align_bytes=64)
             for e in range(2):
                 t = 2 * pair + e
-                look_up(scaled[:, e, :], g_sb[t], first, width, h_sb[t][:, first : first + width], ALU.mult)
+                look_up(scaled[:, e, :], g_sb[t], first, width, h_high[e][first // HALF][:], ALU.mult)
             return scaled
 
         def sums(pair, first, width, scaled, tag):
@@ -262,7 +267,7 @@ def tile_picked_adain8_gelu_po_kernel(
         acc1 = second_product(1, ["y1_1"])
         nc.scalar.copy(o32[0][:], acc0[0][:])
         store(0)
-        u_second = sums(1, HALF, HALF, scaled, "shift3")
+        u_second = sums(1, HALF, HALF, scaled, "h3_0")
         for c in (2, 3):
             gelu(1, c, u_second, HALF)
         round_out(0)

@@ -181,39 +181,37 @@ def tile_picked_adain8_gelu_po_kernel(
         for a in range(2):
             look_up(scaled_low[:, 1, halves[a]], g_sb[1], a * HALF, HALF, h_sb[1][:, halves[a]], ALU.mult)
         shift2 = shift_of(2, rstd2, neg_mean2)
-        h_high = [
-            [keep.tile([P, HALF], F32, name="h%d_%d" % (t, a), tag=tag, align_bytes=64) for a, tag in enumerate(tags)]
-            for t, tags in ((2, ("h0", "raw0")), (3, ("h3_0", "h3_1")))
-        ]
+        h_sb.append(keep.tile([P, S], F32, name="h2", tag="h0", align_bytes=64))
+        h_sb.append(keep.tile([P, S], F32, name="h3", tag="h3", align_bytes=64))
         squares3 = keep.tile([P, S], BF16, name="squares3", tag="g_sb0")
         sum_squares3 = column("sum_squares3", "sum_squares3")
         nc.scalar.activation(squares3[:], y3[:], ACT.Square, bias=neg_mean3[:], accum_out=sum_squares3[:])
-        normalise(h_high[0][0][:], y_half[2][0][:], rstd2, shift2)
+        normalise(h_sb[2][:, halves[0]], y_half[2][0][:], rstd2, shift2)
         rstd3 = column("rstd3", "rstd3")
         nc.scalar.activation(rstd3[:], sum_squares3[:], ACT.Abs_reciprocal_sqrt, bias=EPS, scale=1.0 / S)
-        normalise(h_high[0][1][:], y_half[2][1][:], rstd2, shift2)
+        normalise(h_sb[2][:, halves[1]], y_half[2][1][:], rstd2, shift2)
         shift3 = shift_of(3, rstd3[:], neg_mean3[:])
-        for a in range(2):
-            normalise(h_high[1][a][:], y3[:, halves[a]], rstd3[:], shift3)
+        normalise(h_sb[3][:], y3[:], rstd3[:], shift3)
 
         out_rows = out_0.rearrange("(p t) j -> p t j", t=PACK)
         out_words = out_1[0].rearrange("p n t -> p (n t)").bitcast(I32)
         o_s = keep.tile([P, S], U8, name="o_s", align_bytes=64)
-        z_first = [keep.tile([P, CHUNK, PACK], BF16, name="z%d" % c, tag=tag, align_bytes=64) for c, tag in enumerate(["h3_0", "h0"])]
-        z_sb = [z_first[0][:], z_first[1][:]]
+        u_low = keep.tile([P, 2, S], F32, name="u_low", align_bytes=64)
+        look_up(u_low[:, 0, :], b_sb[0], 0, S, scaled_low[:, 0, :], ALU.subtract)
+        look_up(u_low[:, 1, :], b_sb[1], 0, S, scaled_low[:, 1, :], ALU.add)
+        scaled2 = keep.tile([P, S], F32, name="scaled2")
+        look_up(scaled2[:], g_sb[2], 0, S, h_sb[2][:], ALU.mult)
+        shared = keep.tile([P, 3, HALF], F32, name="shared", align_bytes=64)
+        scaled3 = shared[:, 0:2, :].rearrange("p a j -> p (a j)")
+        look_up(scaled3, g_sb[3], 0, S, h_sb[3][:], ALU.mult)
+        scaled_high = [scaled2[:], scaled3]
+        u_first = keep.tile([P, 2, HALF], F32, name="u_first", align_bytes=64)
+        u_second = shared[:, 0:3:2, :]
+        z_rest = keep.tile([P, 3, CHUNK, PACK], BF16, name="z_rest", align_bytes=64)
+        z_sb = [shared[:, 2, :].bitcast(BF16).rearrange("p (j t) -> p j t", t=PACK)] + [z_rest[:, c, :, :] for c in range(3)]
 
-        def products(pair, first, width, tag):
-            scaled = keep.tile([P, 2, width], F32, name="scaled%d_%d" % (pair, first), tag=tag, align_bytes=64)
-            for e in range(2):
-                t = 2 * pair + e
-                look_up(scaled[:, e, :], g_sb[t], first, width, h_high[e][first // HALF][:], ALU.mult)
-            return scaled
-
-        def sums(pair, first, width, scaled, tag):
-            u = keep.tile([P, 2, width], F32, name="u%d_%d" % (pair, first), tag=tag, align_bytes=64)
-            for e in range(2):
-                look_up(u[:, e, :], b_sb[2 * pair + e], first, width, scaled[:, e, :], ALU.add)
-            return u
+        def add_shift(u, e, a):
+            look_up(u[:, e, :], b_sb[2 + e], a * HALF, HALF, scaled_high[e][:, halves[a]], ALU.add)
 
         def gelu(pair, c, u, first):
             cols = slice(c * CHUNK - first, (c + 1) * CHUNK - first)
@@ -250,44 +248,37 @@ def tile_picked_adain8_gelu_po_kernel(
                 in_=o16[a][:, first : first + count, :, :].rearrange("p c j t -> p (c j t)"),
             )
 
-        u_low = keep.tile([P, 2, S], F32, name="u_low", align_bytes=64)
-        look_up(u_low[:, 0, :], b_sb[0], 0, S, scaled_low[:, 0, :], ALU.subtract)
-        look_up(u_low[:, 1, :], b_sb[1], 0, S, scaled_low[:, 1, :], ALU.add)
-        for c in (0, 1):
+        for c in range(S // CHUNK):
             gelu(0, c, u_low, 0)
-        u_first = sums(1, 0, HALF, products(1, 0, HALF, "scaled1"), "u_first")
+        for e in range(2):
+            add_shift(u_first, e, 0)
         for c in (0, 1):
             gelu(1, c, u_first, 0)
-        z_second = keep.tile([P, 2, CHUNK, PACK], BF16, name="z_second", tag="u_first", align_bytes=64)
-        z_sb.extend([z_second[:, 0, :, :], z_second[:, 1, :, :]])
-        for c in (2, 3):
-            gelu(0, c, u_low, 0)
-        scaled = products(1, HALF, HALF, "scaled1")
+        add_shift(u_second, 0, 1)
         acc0 = second_product(0, ["y1_0"])
         acc1 = second_product(1, ["y1_1"])
-        nc.scalar.copy(o32[0][:], acc0[0][:])
-        store(0)
-        u_second = sums(1, HALF, HALF, scaled, "h3_0")
+        add_shift(u_second, 1, 1)
         for c in (2, 3):
             gelu(1, c, u_second, HALF)
-        round_out(0)
+        nc.vector.tensor_copy(o32[0][:], acc0[0][:])
+        store(0)
         acc2 = second_product(2, ["y2_0"])
-        quantise_out(0, 0, 1)
         acc3 = second_product(3, ["y0_0", "y0_1"])
         nc.scalar.copy(o32[1][:], acc1[0][:])
         store(1)
+        round_out(0)
         round_out(1)
-        quantise_out(0, 1, 1)
-        nc.sync.dma_start(out=out_words[:, halves[0]], in_=o_w[0][:].bitcast(I32))
         nc.scalar.copy(o32[2][:], acc2[0][:])
         store(2)
-        nc.scalar.copy(o32[3][:, 0:2, :], acc3[0][:])
-        nc.vector.tensor_copy(o32[3][:, 2:4, :], acc3[1][:])
+        nc.vector.tensor_copy(o32[3][:, 0:2, :], acc3[0][:])
+        nc.scalar.copy(o32[3][:, 2:4, :], acc3[1][:])
         store(3)
-        round_out(2)
+        quantise_out(0, 0, 2)
+        nc.sync.dma_start(out=out_words[:, halves[0]], in_=o_w[0][:].bitcast(I32))
+        nc.scalar.copy(o16[1][:, 0, :, :], o32[2][:].rearrange("p t j -> p j t"))
         round_out(3)
-        quantise_out(1, 0, 1)
         quantise_out(1, 1, 1)
+        quantise_out(1, 0, 1)
 
         nc.scalar.dma_start(out=out_words[:, halves[1]], in_=o_w[1][:].bitcast(I32))
         for r in range(PACK):

@@ -22,6 +22,7 @@ QUADRANT = 32
 SCALE_ROWS = 16
 HALF = 256
 CHUNK = 128
+W1_ROW, W2_ROW = 4, 8
 EPS = 1e-5
 
 
@@ -54,21 +55,21 @@ def tile_picked_adain8_gelu_po_kernel(
         g_rows = gamma.rearrange("(p t) u -> p t u", t=PACK)
         b_rows = beta.rearrange("(p t) u -> p t u", t=PACK)
 
-        def load_scales(engines, tile, dram):
+        def load_scales(engines, tile, dram, first):
             for r in range(PACK):
                 engines[r].dma_start(
-                    out=tile[r:P:QUADRANT, :].bitcast(I32), in_=dram[0, r:SCALE_ROWS:PACK, :].bitcast(I32)
+                    out=tile[first + r : P : QUADRANT, :].bitcast(I32), in_=dram[0, r:SCALE_ROWS:PACK, :].bitcast(I32)
                 )
 
         nc.sync.dma_start(offs_sb[:], offs)
         nc.sync.dma_start(out=w1_w[:].bitcast(I32), in_=words_of(w1_words))
-        load_scales([nc.scalar, nc.scalar, nc.sync, nc.sync], x_s, x_scales)
+        load_scales([nc.scalar, nc.scalar, nc.sync, nc.sync], x_s, x_scales, 0)
         nc.sync.dma_start(out=x_w[:].bitcast(I32), in_=words_of(x_words))
-        load_scales([nc.sync] * PACK, w1_s, w1_scales)
+        load_scales([nc.sync] * PACK, w1_s, w1_scales, W1_ROW)
         nc.sync.dma_start(out=w2_w[:].bitcast(I32), in_=words_of(w2_words))
         nc.sync.dma_start(sty_sb[:], sty)
         nc.sync.dma_start(out=g_sb[0][:], in_=g_rows[:, 0, :])
-        load_scales([nc.sync] * PACK, w2_s, w2_scales)
+        load_scales([nc.sync] * PACK, w2_s, w2_scales, W2_ROW)
         nc.sync.dma_start(out=g_sb[1][:], in_=g_rows[:, 1, :])
         for t in (0, 1):
             nc.sync.dma_start(out=b_sb[t][:], in_=b_rows[:, t, :])
@@ -85,9 +86,10 @@ def tile_picked_adain8_gelu_po_kernel(
                 out=dst[:].rearrange("p (t m) -> p m t", t=PACK), in_=src[:].rearrange("p (m t) -> p m t", t=PACK)
             )
 
-        def deal_bytes(dst, src):
+        def deal_bytes(dst, src, planes):
             nc.gpsimd.tensor_copy(
-                out=dst[:].rearrange("p (t m) -> p t m", t=PACK), in_=src[:].rearrange("p (m t) -> p t m", t=PACK)
+                out=dst[:].rearrange("p (t m) -> p t m", t=PACK)[:, planes, :],
+                in_=src[:].rearrange("p (m t) -> p t m", t=PACK)[:, planes, :],
             )
 
         halves = [slice(0, HALF), slice(HALF, S)]
@@ -99,25 +101,23 @@ def tile_picked_adain8_gelu_po_kernel(
         for a in range(2):
             nc.vector.tensor_copy(xg_w[a][:], x_w[:].indirect(offs_sb[:, half_lists[a]]))
         w1s_d = keep.tile([P, H], U8, name="w1s_d", align_bytes=64)
-        deal_bytes(w1s_d, w1_s)
+        deal_bytes(w1s_d, w1_s, slice(0, 2))
+        deal_bytes(w1s_d, w1_s, slice(2, 4))
 
         def first_product(out, t, a):
             wc = slice(t * P, (t + 1) * P)
             nc.tensor.matmul_mx(
-                out=out, lhsT=w1_d[:, wc].bitcast(FP8X4), lhsT_scale=w1s_d[:, wc],
+                out=out, lhsT=w1_d[:, wc].bitcast(FP8X4), lhsT_scale=w1s_d[W1_ROW:P, wc],
                 rhs=xg_w[a][:].bitcast(FP8X4), rhs_scale=xg_s[:, halves[a]], start=True, stop=True,
             )
 
         y_half = [[psum.tile([P, HALF], F32, name="y%d_%d" % (t, a), tag="y%d_%d" % (t, a)) for a in range(2)] for t in range(3)]
         y3 = psum.tile([P, S], F32, name="y3", tag="y3")
-        for t in range(3):
-            for a in range(2):
-                first_product(y_half[t][a][:], t, a)
+        for t, a in ((0, 0), (1, 0), (0, 1), (1, 1), (2, 0), (2, 1)):
+            first_product(y_half[t][a][:], t, a)
         for a in range(2):
             first_product(y3[:, halves[a]], 3, a)
 
-        w2_d = keep.tile([P, N], U32, name="w2_d", tag="x_w", align_bytes=64)
-        deal(w2_d, w2_w)
         stats = [keep.tile([P, 2, 6], F32, name="stats%d" % t, tag="stats%d" % t, align_bytes=64) for t in range(3)]
         moments = [keep.tile([P, 2], F32, name="mv%d" % t, tag="mv%d" % t, align_bytes=64) for t in range(3)]
 
@@ -128,16 +128,18 @@ def tile_picked_adain8_gelu_po_kernel(
             nc.vector.bn_aggr(moments[t][:], stats[t][:].rearrange("p a s -> p (a s)"))
 
         half_stats(0, 0)
-        half_stats(0, 1)
         half_stats(1, 0)
-        aggregate(0)
+        half_stats(0, 1)
         half_stats(1, 1)
+        aggregate(0)
         half_stats(2, 0)
         aggregate(1)
         half_stats(2, 1)
+        w2_d = keep.tile([P, N], U32, name="w2_d", tag="stats0", align_bytes=64)
+        deal(w2_d, w2_w)
         aggregate(2)
         w2s_d = keep.tile([P, N], U8, name="w2s_d", align_bytes=64)
-        deal_bytes(w2s_d, w2_s)
+        deal_bytes(w2s_d, w2_s, slice(0, 4))
 
         h_sb = [keep.tile([P, S], F32, name="h%d" % t, tag="h%d" % t, align_bytes=64) for t in range(2)]
 
@@ -205,10 +207,12 @@ def tile_picked_adain8_gelu_po_kernel(
         scaled3 = shared[:, 0:2, :].rearrange("p a j -> p (a j)")
         look_up(scaled3, g_sb[3], 0, S, h_sb[3][:], ALU.mult)
         scaled_high = [scaled2[:], scaled3]
-        u_first = keep.tile([P, 2, HALF], F32, name="u_first", align_bytes=64)
+        late = keep.tile([P, S + 3 * CHUNK], F32, name="late", align_bytes=64)
+        u_first = late[:, 3 * CHUNK :].rearrange("p (e j) -> p e j", e=2)
+        z_late = late[:, 0:S].bitcast(BF16).rearrange("p (j t) -> p j t", t=PACK)
         u_second = shared[:, 0:3:2, :]
-        z_rest = keep.tile([P, 3, CHUNK, PACK], BF16, name="z_rest", align_bytes=64)
-        z_sb = [shared[:, 2, :].bitcast(BF16).rearrange("p (j t) -> p j t", t=PACK)] + [z_rest[:, c, :, :] for c in range(3)]
+        z_one = keep.tile([P, CHUNK, PACK], BF16, name="z_one", align_bytes=64)
+        z_sb = [shared[:, 2, :].bitcast(BF16).rearrange("p (j t) -> p j t", t=PACK)] + [z_one[:], z_late[:, 0:CHUNK, :], z_late[:, CHUNK:HALF, :]]
 
         def add_shift(u, e, a):
             look_up(u[:, e, :], b_sb[2 + e], a * HALF, HALF, scaled_high[e][:, halves[a]], ALU.add)
@@ -226,7 +230,7 @@ def tile_picked_adain8_gelu_po_kernel(
             for t in range(PACK):
                 wc = slice(t * P, (t + 1) * P)
                 nc.tensor.matmul_mx(
-                    out=banks[t // per_bank][:, t % per_bank, :], lhsT=w2_d[:, wc].bitcast(FP8X4), lhsT_scale=w2s_d[:, wc],
+                    out=banks[t // per_bank][:, t % per_bank, :], lhsT=w2_d[:, wc].bitcast(FP8X4), lhsT_scale=w2s_d[W2_ROW:P, wc],
                     rhs=z_w[:].bitcast(FP8X4), rhs_scale=z_s[:], start=True, stop=True,
                 )
             return banks
@@ -248,12 +252,13 @@ def tile_picked_adain8_gelu_po_kernel(
                 in_=o16[a][:, first : first + count, :, :].rearrange("p c j t -> p (c j t)"),
             )
 
-        for c in range(S // CHUNK):
+        for c in (0, 1):
             gelu(0, c, u_low, 0)
         for e in range(2):
             add_shift(u_first, e, 0)
         for c in (0, 1):
             gelu(1, c, u_first, 0)
+        nc.scalar.activation(z_late[:, :, 0:2], u_low[:, :, halves[1]].rearrange("p e j -> p j e"), ACT.Gelu_apprx_tanh)
         add_shift(u_second, 0, 1)
         acc0 = second_product(0, ["y1_0"])
         acc1 = second_product(1, ["y1_1"])

@@ -66,17 +66,17 @@ def tile_picked_adain8_gelu_po_kernel(
         load_scales([nc.scalar, nc.scalar, nc.sync, nc.sync], x_s, x_scales, 0)
         nc.sync.dma_start(out=x_w[:].bitcast(I32), in_=words_of(x_words))
         load_scales([nc.sync] * PACK, w1_s, w1_scales, W1_ROW)
-        nc.sync.dma_start(out=w2_w[:].bitcast(I32), in_=words_of(w2_words))
         nc.sync.dma_start(sty_sb[:], sty)
-        nc.sync.dma_start(out=g_sb[0][:], in_=g_rows[:, 0, :])
+        for t in (0, 1):
+            nc.sync.dma_start(out=g_sb[t][:], in_=g_rows[:, t, :])
         load_scales([nc.sync] * PACK, w2_s, w2_scales, W2_ROW)
-        nc.sync.dma_start(out=g_sb[1][:], in_=g_rows[:, 1, :])
         for t in (0, 1):
             nc.sync.dma_start(out=b_sb[t][:], in_=b_rows[:, t, :])
         for t in (2, 3):
             nc.sync.dma_start(out=g_sb[t][:], in_=g_rows[:, t, :])
         for t in (2, 3):
             nc.sync.dma_start(out=b_sb[t][:], in_=b_rows[:, t, :])
+        nc.sync.dma_start(out=w2_w[:].bitcast(I32), in_=words_of(w2_words))
 
         xg_s = keep.tile([P, S], U8, name="xg_s", align_bytes=64)
         w1_d = keep.tile([P, H], U32, name="w1_d", align_bytes=64)
@@ -135,8 +135,6 @@ def tile_picked_adain8_gelu_po_kernel(
         half_stats(2, 0)
         aggregate(1)
         half_stats(2, 1)
-        w2_d = keep.tile([P, N], U32, name="w2_d", tag="stats0", align_bytes=64)
-        deal(w2_d, w2_w)
         aggregate(2)
         w2s_d = keep.tile([P, N], U8, name="w2s_d", align_bytes=64)
         deal_bytes(w2s_d, w2_s, slice(0, 4))
@@ -164,35 +162,41 @@ def tile_picked_adain8_gelu_po_kernel(
             lists = sty_sb[:, first // GROUP : (first + width) // GROUP]
             nc.vector.tensor_tensor(out, table[:].indirect(lists), other, op)
 
-        rstd0 = column("rstd0", "rstd0")[:]
-        nc.scalar.activation(rstd0, moments[0][:, 1:2], ACT.Abs_reciprocal_sqrt, bias=EPS)
+        def rstd_of(t):
+            rstd = column("rstd%d" % t, "rstd%d" % t)
+            nc.scalar.activation(rstd[:], moments[t][:, 1:2], ACT.Abs_reciprocal_sqrt, bias=EPS)
+            return rstd[:]
+
+        def centre(t):
+            for a in range(2):
+                nc.scalar.activation(h_sb[t][:, halves[a]], y_half[t][a][:], ACT.Identity, bias=moments[t][:, 0:1], scale=-1.0)
+
+        raw = [keep.tile([P, S], F32, name="raw%d" % t, tag="raw%d" % t, align_bytes=64) for t in range(2)]
+        scaled_low = keep.tile([P, 2, S], F32, name="scaled_low")
+        rstd0 = rstd_of(0)
+        centre(0)
         for a in range(2):
-            nc.scalar.activation(h_sb[0][:, halves[a]], y_half[0][a][:], ACT.Identity, bias=moments[0][:, 0:1], scale=-1.0)
-        raw0 = keep.tile([P, S], F32, name="raw0", tag="raw0", align_bytes=64)
-        look_up(raw0[:], g_sb[0], 0, S, h_sb[0][:], ALU.mult)
-        rstd1, neg_mean1 = scale_of(1, "both1")
+            look_up(raw[0][:, halves[a]], g_sb[0], a * HALF, HALF, h_sb[0][:, halves[a]], ALU.mult)
+        centre(1)
+        look_up(raw[1][:], g_sb[1], 0, S, h_sb[1][:], ALU.mult)
+        rstd1 = rstd_of(1)
         neg_mean3 = column("neg_mean3", "neg_mean3")
         terms3 = keep.tile([P, S], BF16, name="terms3", tag="stats1", align_bytes=64)
         nc.scalar.activation(terms3[:], y3[:], ACT.Copy, scale=-1.0 / S, accum_out=neg_mean3[:])
-        shift1 = shift_of(1, rstd1, neg_mean1)
         rstd2, neg_mean2 = scale_of(2, "both2")
-        for a in range(2):
-            normalise(h_sb[1][:, halves[a]], y_half[1][a][:], rstd1, shift1)
-        scaled_low = keep.tile([P, 2, S], F32, name="scaled_low")
-        nc.scalar.activation(scaled_low[:, 0, :], raw0[:], ACT.Identity, scale=rstd0)
-        for a in range(2):
-            look_up(scaled_low[:, 1, halves[a]], g_sb[1], a * HALF, HALF, h_sb[1][:, halves[a]], ALU.mult)
+        nc.scalar.activation(scaled_low[:, 0, :], raw[0][:], ACT.Identity, scale=rstd0)
         shift2 = shift_of(2, rstd2, neg_mean2)
-        h_sb.append(keep.tile([P, S], F32, name="h2", tag="h0", align_bytes=64))
+        h_sb.append(keep.tile([P, S], F32, name="h2", tag="h1", align_bytes=64))
         h_sb.append(keep.tile([P, S], F32, name="h3", tag="h3", align_bytes=64))
         squares3 = keep.tile([P, S], BF16, name="squares3", tag="g_sb0")
         sum_squares3 = column("sum_squares3", "sum_squares3")
         nc.scalar.activation(squares3[:], y3[:], ACT.Square, bias=neg_mean3[:], accum_out=sum_squares3[:])
-        normalise(h_sb[2][:, halves[0]], y_half[2][0][:], rstd2, shift2)
+        nc.scalar.activation(scaled_low[:, 1, :], raw[1][:], ACT.Identity, scale=rstd1)
         rstd3 = column("rstd3", "rstd3")
         nc.scalar.activation(rstd3[:], sum_squares3[:], ACT.Abs_reciprocal_sqrt, bias=EPS, scale=1.0 / S)
-        normalise(h_sb[2][:, halves[1]], y_half[2][1][:], rstd2, shift2)
+        normalise(h_sb[2][:, halves[0]], y_half[2][0][:], rstd2, shift2)
         shift3 = shift_of(3, rstd3[:], neg_mean3[:])
+        normalise(h_sb[2][:, halves[1]], y_half[2][1][:], rstd2, shift2)
         normalise(h_sb[3][:], y3[:], rstd3[:], shift3)
 
         out_rows = out_0.rearrange("(p t) j -> p t j", t=PACK)
@@ -200,7 +204,7 @@ def tile_picked_adain8_gelu_po_kernel(
         o_s = keep.tile([P, S], U8, name="o_s", align_bytes=64)
         u_low = keep.tile([P, 2, S], F32, name="u_low", align_bytes=64)
         look_up(u_low[:, 0, :], b_sb[0], 0, S, scaled_low[:, 0, :], ALU.subtract)
-        look_up(u_low[:, 1, :], b_sb[1], 0, S, scaled_low[:, 1, :], ALU.add)
+        look_up(u_low[:, 1, :], b_sb[1], 0, S, scaled_low[:, 1, :], ALU.subtract)
         scaled2 = keep.tile([P, S], F32, name="scaled2")
         look_up(scaled2[:], g_sb[2], 0, S, h_sb[2][:], ALU.mult)
         shared = keep.tile([P, 3, HALF], F32, name="shared", align_bytes=64)
@@ -259,6 +263,8 @@ def tile_picked_adain8_gelu_po_kernel(
         for c in (0, 1):
             gelu(1, c, u_first, 0)
         nc.scalar.activation(z_late[:, :, 0:2], u_low[:, :, halves[1]].rearrange("p e j -> p j e"), ACT.Gelu_apprx_tanh)
+        w2_d = keep.tile([P, N], U32, name="w2_d", align_bytes=64)
+        deal(w2_d, w2_w)
         add_shift(u_second, 0, 1)
         acc0 = second_product(0, ["y1_0"])
         acc1 = second_product(1, ["y1_1"])

@@ -47,7 +47,7 @@ def tile_picked_adain8_gelu_po_kernel(
         w2_w = keep.tile([P, N], U32, name="w2_w", align_bytes=64)
         w1_s = keep.tile([P, H], U8, name="w1_s", tag="w1_s", align_bytes=64)
         g_sb = [keep.tile([P, U], F32, name="g_sb%d" % t, tag="g_sb%d" % t) for t in range(PACK)]
-        b_sb = [keep.tile([P, U], F32, name="b_sb%d" % t) for t in range(PACK)]
+        b_sb = [keep.tile([P, U], F32, name="b_sb%d" % t, tag="b_sb%d" % t, align_bytes=64) for t in range(PACK)]
 
         for scale_tile in (x_s, w1_s, w2_s):
             nc.vector.memset(scale_tile[:].bitcast(I32), 0)
@@ -111,35 +111,37 @@ def tile_picked_adain8_gelu_po_kernel(
                 rhs=xg_w[a][:].bitcast(FP8X4), rhs_scale=xg_s[:, halves[a]], start=True, stop=True,
             )
 
-        y_half = [[psum.tile([P, HALF], F32, name="y%d_%d" % (t, a), tag="y%d_%d" % (t, a)) for a in range(2)] for t in range(3)]
+        y_half = [[psum.tile([P, HALF], F32, name="y%d_%d" % (t, a), tag="y%d_%d" % (t, a)) for a in range(2)] for t in range(2)]
+        y2 = psum.tile([P, S], F32, name="y2", tag="y2")
         y3 = psum.tile([P, S], F32, name="y3", tag="y3")
-        for t, a in ((0, 0), (1, 0), (0, 1), (1, 1), (2, 0), (2, 1)):
-            first_product(y_half[t][a][:], t, a)
         for a in range(2):
-            first_product(y3[:, halves[a]], 3, a)
+            for t in range(2):
+                first_product(y_half[t][a][:], t, a)
+        for t, y in ((2, y2), (3, y3)):
+            for a in range(2):
+                first_product(y[:, halves[a]], t, a)
 
-        stats = [keep.tile([P, 2, 6], F32, name="stats%d" % t, tag="stats%d" % t, align_bytes=64) for t in range(3)]
-        moments = [keep.tile([P, 2], F32, name="mv%d" % t, tag="mv%d" % t, align_bytes=64) for t in range(3)]
+        stats = [keep.tile([P, 2, 6], F32, name="stats%d" % t, tag="stats%d" % t, align_bytes=64) for t in range(2)]
+        stats2 = keep.tile([P, 6], F32, name="stats2", align_bytes=64)
+        h_sb = [keep.tile([P, S], F32, name="h%d" % t, tag="h%d" % t, align_bytes=64) for t in range(2)]
+        moments = [keep.tile([P, 2], F32, name="mv%d" % t, tag="mv%d" % t, align_bytes=64)[:] for t in range(2)]
+        moments.append(h_sb[0][:, 0:2])
 
         def half_stats(t, a):
             nc.vector.bn_stats(stats[t][:, a, :], y_half[t][a][:])
 
         def aggregate(t):
-            nc.vector.bn_aggr(moments[t][:], stats[t][:].rearrange("p a s -> p (a s)"))
+            nc.vector.bn_aggr(moments[t], stats[t][:].rearrange("p a s -> p (a s)"))
 
         half_stats(0, 0)
         half_stats(1, 0)
         half_stats(0, 1)
         half_stats(1, 1)
         aggregate(0)
-        half_stats(2, 0)
+        nc.vector.bn_stats(stats2[:], y2[:])
         aggregate(1)
-        half_stats(2, 1)
-        aggregate(2)
         w2s_d = keep.tile([P, N], U8, name="w2s_d", align_bytes=64)
         deal_bytes(w2s_d, w2_s, slice(0, 4))
-
-        h_sb = [keep.tile([P, S], F32, name="h%d" % t, tag="h%d" % t, align_bytes=64) for t in range(2)]
 
         def column(name, tag):
             return keep.tile([P, 1], F32, name=name, tag=tag, align_bytes=64)
@@ -177,6 +179,7 @@ def tile_picked_adain8_gelu_po_kernel(
         centre(0)
         for a in range(2):
             look_up(raw[0][:, halves[a]], g_sb[0], a * HALF, HALF, h_sb[0][:, halves[a]], ALU.mult)
+        nc.vector.bn_aggr(moments[2], stats2[:])
         centre(1)
         look_up(raw[1][:], g_sb[1], 0, S, h_sb[1][:], ALU.mult)
         rstd1 = rstd_of(1)
@@ -194,9 +197,8 @@ def tile_picked_adain8_gelu_po_kernel(
         nc.scalar.activation(scaled_low[:, 1, :], raw[1][:], ACT.Identity, scale=rstd1)
         rstd3 = column("rstd3", "rstd3")
         nc.scalar.activation(rstd3[:], sum_squares3[:], ACT.Abs_reciprocal_sqrt, bias=EPS, scale=1.0 / S)
-        normalise(h_sb[2][:, halves[0]], y_half[2][0][:], rstd2, shift2)
+        normalise(h_sb[2][:], y2[:], rstd2, shift2)
         shift3 = shift_of(3, rstd3[:], neg_mean3[:])
-        normalise(h_sb[2][:, halves[1]], y_half[2][1][:], rstd2, shift2)
         normalise(h_sb[3][:], y3[:], rstd3[:], shift3)
 
         out_rows = out_0.rearrange("(p t) j -> p t j", t=PACK)
@@ -207,19 +209,19 @@ def tile_picked_adain8_gelu_po_kernel(
         look_up(u_low[:, 1, :], b_sb[1], 0, S, scaled_low[:, 1, :], ALU.subtract)
         scaled2 = keep.tile([P, S], F32, name="scaled2")
         look_up(scaled2[:], g_sb[2], 0, S, h_sb[2][:], ALU.mult)
-        shared = keep.tile([P, 3, HALF], F32, name="shared", align_bytes=64)
-        scaled3 = shared[:, 0:2, :].rearrange("p a j -> p (a j)")
-        look_up(scaled3, g_sb[3], 0, S, h_sb[3][:], ALU.mult)
-        scaled_high = [scaled2[:], scaled3]
-        late = keep.tile([P, S + 3 * CHUNK], F32, name="late", align_bytes=64)
+        scaled3 = keep.tile([P, HALF], F32, name="scaled3")
+        look_up(scaled3[:], g_sb[3], 0, HALF, h_sb[3][:, halves[0]], ALU.mult)
+        late = keep.tile([P, 7 * CHUNK], F32, name="late", align_bytes=64)
         u_first = late[:, 3 * CHUNK :].rearrange("p (e j) -> p e j", e=2)
         z_late = late[:, 0:S].bitcast(BF16).rearrange("p (j t) -> p j t", t=PACK)
-        u_second = shared[:, 0:3:2, :]
-        z_one = keep.tile([P, CHUNK, PACK], BF16, name="z_one", align_bytes=64)
-        z_sb = [shared[:, 2, :].bitcast(BF16).rearrange("p (j t) -> p j t", t=PACK)] + [z_one[:], z_late[:, 0:CHUNK, :], z_late[:, CHUNK:HALF, :]]
+        early = keep.tile([P, S], F32, name="early", align_bytes=64)
+        u_second = early[:].rearrange("p (e j) -> p e j", e=2)
+        z_early = early[:].bitcast(BF16).rearrange("p (j t) -> p j t", t=PACK)
+        z_sb = [z[:, c * CHUNK : (c + 1) * CHUNK, :] for z in (z_early, z_late) for c in range(2)]
 
         def add_shift(u, e, a):
-            look_up(u[:, e, :], b_sb[2 + e], a * HALF, HALF, scaled_high[e][:, halves[a]], ALU.add)
+            scaled = scaled3[:] if e else scaled2[:, halves[a]]
+            look_up(u[:, e, :], b_sb[2 + e], a * HALF, HALF, scaled, ALU.add)
 
         def gelu(pair, c, u, first):
             cols = slice(c * CHUNK - first, (c + 1) * CHUNK - first)
@@ -240,7 +242,7 @@ def tile_picked_adain8_gelu_po_kernel(
             return banks
 
         o32 = [keep.tile([P, PACK, CHUNK], F32, name="o32_%d" % c) for c in range(S // CHUNK)]
-        o16 = [keep.tile([P, 2, CHUNK, PACK], BF16, name="o16_%d" % a, align_bytes=64) for a in range(2)]
+        o16 = [keep.tile([P, 2, CHUNK, PACK], BF16, name="o16_%d" % a, tag=tag, align_bytes=64) for a, tag in enumerate(("b_sb2", "o16_1"))]
         o_w = [keep.tile([P, HALF], U32, name="o_w%d" % a, align_bytes=64) for a in range(2)]
 
         def store(c):
@@ -265,31 +267,33 @@ def tile_picked_adain8_gelu_po_kernel(
         nc.scalar.activation(z_late[:, :, 0:2], u_low[:, :, halves[1]].rearrange("p e j -> p j e"), ACT.Gelu_apprx_tanh)
         w2_d = keep.tile([P, N], U32, name="w2_d", align_bytes=64)
         deal(w2_d, w2_w)
-        add_shift(u_second, 0, 1)
+        look_up(scaled3[:], g_sb[3], HALF, HALF, h_sb[3][:, halves[1]], ALU.mult)
         acc0 = second_product(0, ["y1_0"])
         acc1 = second_product(1, ["y1_1"])
-        add_shift(u_second, 1, 1)
+        for e in range(2):
+            add_shift(u_second, e, 1)
+        nc.scalar.copy(o32[0][:], acc0[0][:])
+        store(0)
         for c in (2, 3):
             gelu(1, c, u_second, HALF)
-        nc.vector.tensor_copy(o32[0][:], acc0[0][:])
-        store(0)
-        acc2 = second_product(2, ["y2_0"])
-        acc3 = second_product(3, ["y0_0", "y0_1"])
-        nc.scalar.copy(o32[1][:], acc1[0][:])
+        nc.vector.tensor_copy(o32[1][:], acc1[0][:])
         store(1)
+        acc2 = second_product(2, ["y2", "y3"])
         round_out(0)
+        acc3 = second_product(3, ["y0_0", "y0_1"])
         round_out(1)
-        nc.scalar.copy(o32[2][:], acc2[0][:])
+        quantise_out(0, 0, 2)
+        nc.sync.dma_start(out=out_words[:, halves[0]], in_=o_w[0][:].bitcast(I32))
+        nc.scalar.copy(o32[2][:, 0:2, :], acc2[0][:])
+        nc.scalar.copy(o32[2][:, 2:4, :], acc2[1][:])
         store(2)
         nc.vector.tensor_copy(o32[3][:, 0:2, :], acc3[0][:])
         nc.scalar.copy(o32[3][:, 2:4, :], acc3[1][:])
         store(3)
-        quantise_out(0, 0, 2)
-        nc.sync.dma_start(out=out_words[:, halves[0]], in_=o_w[0][:].bitcast(I32))
-        nc.scalar.copy(o16[1][:, 0, :, :], o32[2][:].rearrange("p t j -> p j t"))
+        round_out(2)
         round_out(3)
-        quantise_out(1, 1, 1)
         quantise_out(1, 0, 1)
+        quantise_out(1, 1, 1)
 
         nc.scalar.dma_start(out=out_words[:, halves[1]], in_=o_w[1][:].bitcast(I32))
         for r in range(PACK):

@@ -42,7 +42,7 @@ def tile_picked_adain8_gelu_po_kernel(
         sty_sb = keep.tile([P, S // GROUP], U16, name="sty_sb")
         x_w = keep.tile([P, T], U32, name="x_w", tag="x_w", align_bytes=64)
         x_s = keep.tile([P, T], U8, name="x_s", align_bytes=64)
-        w2_s = keep.tile([P, N], U8, name="w2_s", align_bytes=64)
+        w2_s = keep.tile([P, N], U8, name="w2_s", tag="spread0", align_bytes=64)
         w1_w = keep.tile([P, H], U32, name="w1_w", align_bytes=64)
         w2_w = keep.tile([P, N], U32, name="w2_w", align_bytes=64)
         w1_s = keep.tile([P, H], U8, name="w1_s", tag="w1_s", align_bytes=64)
@@ -51,6 +51,11 @@ def tile_picked_adain8_gelu_po_kernel(
 
         for scale_tile in (x_s, w1_s, w2_s):
             nc.vector.memset(scale_tile[:].bitcast(I32), 0)
+
+        one = keep.tile([P, 2], F32, name="one", align_bytes=64)
+        nc.vector.memset(one[:], 1.0)
+        power = keep.tile([P, 2], F32, name="power", align_bytes=64)
+        nc.gpsimd.tensor_scalar(power[:], one[:], -0.5, None, ALU.mult)
 
         g_rows = gamma.rearrange("(p t) u -> p t u", t=PACK)
         b_rows = beta.rearrange("(p t) u -> p t u", t=PACK)
@@ -65,6 +70,8 @@ def tile_picked_adain8_gelu_po_kernel(
         nc.sync.dma_start(out=w1_w[:].bitcast(I32), in_=words_of(w1_words))
         load_scales([nc.scalar, nc.scalar, nc.sync, nc.sync], x_s, x_scales, 0)
         nc.sync.dma_start(out=x_w[:].bitcast(I32), in_=words_of(x_words))
+        unread = keep.tile([P, 1], F32, name="unread", align_bytes=64)
+        nc.scalar.activation(unread[:], one[:, 0:1], ACT.Gelu_apprx_tanh)
         load_scales([nc.sync] * PACK, w1_s, w1_scales, W1_ROW)
         nc.sync.dma_start(sty_sb[:], sty)
         for t in (0, 1):
@@ -111,126 +118,124 @@ def tile_picked_adain8_gelu_po_kernel(
                 rhs=xg_w[a][:].bitcast(FP8X4), rhs_scale=xg_s[:, halves[a]], start=True, stop=True,
             )
 
-        y_half = [[psum.tile([P, HALF], F32, name="y%d_%d" % (t, a), tag="y%d_%d" % (t, a)) for a in range(2)] for t in range(2)]
-        y2 = psum.tile([P, S], F32, name="y2", tag="y2")
-        y3 = psum.tile([P, S], F32, name="y3", tag="y3")
+        y_half = {t: [psum.tile([P, HALF], F32, name="y%d_%d" % (t, a), tag="y%d_%d" % (t, a)) for a in range(2)] for t in (0, 1)}
+        y_whole = {t: psum.tile([P, S], F32, name="y%d" % t, tag="y%d" % t) for t in (2, 3)}
         for a in range(2):
-            for t in range(2):
+            for t in (0, 1):
                 first_product(y_half[t][a][:], t, a)
-        for t, y in ((2, y2), (3, y3)):
+        for t in (2, 3):
             for a in range(2):
-                first_product(y[:, halves[a]], t, a)
+                first_product(y_whole[t][:, halves[a]], t, a)
 
-        stats = [keep.tile([P, 2, 6], F32, name="stats%d" % t, tag="stats%d" % t, align_bytes=64) for t in range(2)]
-        stats2 = keep.tile([P, 6], F32, name="stats2", align_bytes=64)
-        h_sb = [keep.tile([P, S], F32, name="h%d" % t, tag="h%d" % t, align_bytes=64) for t in range(2)]
-        moments = [keep.tile([P, 2], F32, name="mv%d" % t, tag="mv%d" % t, align_bytes=64)[:] for t in range(2)]
-        moments.append(h_sb[0][:, 0:2])
+        def plane(name):
+            return keep.tile([P, S], F32, name=name, tag=name, align_bytes=64)
 
-        def half_stats(t, a):
-            nc.vector.bn_stats(stats[t][:, a, :], y_half[t][a][:])
+        def columns(name, count):
+            return keep.tile([P, count], F32, name=name, tag=name, align_bytes=64)
+
+        def fetch(name, table, tag=None):
+            picked = keep.tile([P, S], F32, name=name, tag=tag or name, align_bytes=64)
+            nc.scalar.activation(picked[:], table[:].indirect(sty_sb[:]), ACT.Copy)
+            return picked
+
+        def look_up(out, table, a, other, op):
+            nc.vector.tensor_tensor(out, table[:].indirect(sty_sb[:, half_lists[a]]), other, op)
+
+        gain = [fetch("gain0", g_sb[0]), fetch("gain1", g_sb[1])]
+        shift = [fetch("shift0", b_sb[0]), fetch("shift1", b_sb[1])]
+
+        stats = {t: keep.tile([P, 2, 6], F32, name="stats%d" % t, align_bytes=64) for t in (0, 1)}
+        for t in (2, 3):
+            stats[t] = columns("stats%d" % t, 6)
+        pairs = ((0, 1), (2, 3))
+        moments = [keep.tile([P, 2, 2], F32, name="moments%d" % e, align_bytes=64) for e in range(2)]
+        moment_of = {t: moments[e][:, i, :] for e, pair in enumerate(pairs) for i, t in enumerate(pair)}
+        rstd = {}
+
+        def mean_of(t):
+            return moment_of[t][:, 0:1]
 
         def aggregate(t):
-            nc.vector.bn_aggr(moments[t], stats[t][:].rearrange("p a s -> p (a s)"))
+            src = stats[t][:].rearrange("p a s -> p (a s)") if t in y_half else stats[t][:]
+            nc.vector.bn_aggr(moment_of[t], src)
 
-        half_stats(0, 0)
-        half_stats(1, 0)
-        half_stats(0, 1)
-        half_stats(1, 1)
-        aggregate(0)
-        nc.vector.bn_stats(stats2[:], y2[:])
-        aggregate(1)
+        def rstd_of(e):
+            spread = keep.tile([P, 2], F32, name="spread%d" % e, tag="spread0", align_bytes=64)
+            nc.gpsimd.tensor_scalar(spread[:], moments[e][:, :, 1], EPS, None, ALU.add)
+            both = columns("rstd%d" % e, 2)
+            nc.gpsimd.tensor_tensor(both[:], spread[:], power[:], ALU.pow)
+            for i, t in enumerate(pairs[e]):
+                rstd[t] = both[:, i : i + 1]
+
         w2s_d = keep.tile([P, N], U8, name="w2s_d", align_bytes=64)
         deal_bytes(w2s_d, w2_s, slice(0, 4))
-
-        def column(name, tag):
-            return keep.tile([P, 1], F32, name=name, tag=tag, align_bytes=64)
-
-        def scale_of(t, tag):
-            both = keep.tile([P, 2], F32, name="rstd_neg_mean%d" % t, tag=tag, align_bytes=64)
-            nc.scalar.activation(both[:, 0:1], moments[t][:, 1:2], ACT.Abs_reciprocal_sqrt, bias=EPS)
-            nc.scalar.activation(both[:, 1:2], moments[t][:, 0:1], ACT.Identity, scale=-1.0)
-            return both[:, 0:1], both[:, 1:2]
-
-        def shift_of(t, rstd, neg_mean):
-            shift = column("shift%d" % t, "shift%d" % t)
-            nc.scalar.activation(shift[:], neg_mean, ACT.Identity, scale=rstd)
-            return shift[:]
-
-        def normalise(out, y, rstd, shift):
-            nc.scalar.activation(out, y, ACT.Identity, bias=shift, scale=rstd)
-
-        def look_up(out, table, first, width, other, op):
-            lists = sty_sb[:, first // GROUP : (first + width) // GROUP]
-            nc.vector.tensor_tensor(out, table[:].indirect(lists), other, op)
-
-        def rstd_of(t):
-            rstd = column("rstd%d" % t, "rstd%d" % t)
-            nc.scalar.activation(rstd[:], moments[t][:, 1:2], ACT.Abs_reciprocal_sqrt, bias=EPS)
-            return rstd[:]
-
-        def centre(t):
-            for a in range(2):
-                nc.scalar.activation(h_sb[t][:, halves[a]], y_half[t][a][:], ACT.Identity, bias=moments[t][:, 0:1], scale=-1.0)
-
-        raw = [keep.tile([P, S], F32, name="raw%d" % t, tag="raw%d" % t, align_bytes=64) for t in range(2)]
-        scaled_low = keep.tile([P, 2, S], F32, name="scaled_low")
-        rstd0 = rstd_of(0)
-        centre(0)
         for a in range(2):
-            look_up(raw[0][:, halves[a]], g_sb[0], a * HALF, HALF, h_sb[0][:, halves[a]], ALU.mult)
-        nc.vector.bn_aggr(moments[2], stats2[:])
-        centre(1)
-        look_up(raw[1][:], g_sb[1], 0, S, h_sb[1][:], ALU.mult)
-        rstd1 = rstd_of(1)
-        neg_mean3 = column("neg_mean3", "neg_mean3")
-        terms3 = keep.tile([P, S], BF16, name="terms3", tag="stats1", align_bytes=64)
-        nc.scalar.activation(terms3[:], y3[:], ACT.Copy, scale=-1.0 / S, accum_out=neg_mean3[:])
-        rstd2, neg_mean2 = scale_of(2, "both2")
-        nc.scalar.activation(scaled_low[:, 0, :], raw[0][:], ACT.Identity, scale=rstd0)
-        shift2 = shift_of(2, rstd2, neg_mean2)
-        h_sb.append(keep.tile([P, S], F32, name="h2", tag="h1", align_bytes=64))
-        h_sb.append(keep.tile([P, S], F32, name="h3", tag="h3", align_bytes=64))
-        squares3 = keep.tile([P, S], BF16, name="squares3", tag="g_sb0")
-        sum_squares3 = column("sum_squares3", "sum_squares3")
-        nc.scalar.activation(squares3[:], y3[:], ACT.Square, bias=neg_mean3[:], accum_out=sum_squares3[:])
-        nc.scalar.activation(scaled_low[:, 1, :], raw[1][:], ACT.Identity, scale=rstd1)
-        rstd3 = column("rstd3", "rstd3")
-        nc.scalar.activation(rstd3[:], sum_squares3[:], ACT.Abs_reciprocal_sqrt, bias=EPS, scale=1.0 / S)
-        normalise(h_sb[2][:], y2[:], rstd2, shift2)
-        shift3 = shift_of(3, rstd3[:], neg_mean3[:])
-        normalise(h_sb[3][:], y3[:], rstd3[:], shift3)
+            for t in (0, 1):
+                nc.vector.bn_stats(stats[t][:, a, :], y_half[t][a][:])
+        aggregate(0)
+        nc.vector.bn_stats(stats[2][:], y_whole[2][:])
+        aggregate(1)
+        rstd_of(0)
+        nc.vector.bn_stats(stats[3][:], y_whole[3][:])
+        aggregate(2)
+
+        prod = [plane("prod%d" % t) for t in range(3)]
+        prod3 = keep.tile([P, HALF], F32, name="prod3", align_bytes=64)
+
+        def centre_and_gain(t, a):
+            nc.vector.scalar_tensor_tensor(prod[t][:, halves[a]], y_half[t][a][:], mean_of(t), gain[t][:, halves[a]], ALU.subtract, ALU.mult)
+
+        centre_and_gain(0, 0)
+        aggregate(3)
+        rstd_of(1)
+        offset = {t: columns("offset%d" % t, 1) for t in (2, 3)}
+        for t in (2, 3):
+            nc.gpsimd.tensor_scalar(offset[t][:], mean_of(t), rstd[t], -1.0, ALU.mult, ALU.mult)
+        centre_and_gain(0, 1)
+        for a in range(2):
+            centre_and_gain(1, a)
+
+        u_low = keep.tile([P, 2, S], F32, name="u_low", align_bytes=64)
+
+        def scale_and_shift(out, t, cols):
+            nc.vector.scalar_tensor_tensor(out, prod[t][:, cols], rstd[t], shift[t][:, cols], ALU.mult, ALU.add)
+
+        for t in range(2):
+            scale_and_shift(u_low[:, t, :], t, slice(0, S))
+        h_high = keep.tile([P, 2, S], F32, name="h_high", tag="b_sb1", align_bytes=64)
+        for t in (2, 3):
+            nc.scalar.activation(h_high[:, t - 2, :], y_whole[t][:], ACT.Identity, bias=offset[t][:], scale=rstd[t])
+        shift.append(fetch("shift2", b_sb[2], "offset2"))
+        nc.vector.tensor_tensor(prod[2][:], g_sb[2][:].indirect(sty_sb[:]), h_high[:, 0, :], ALU.mult)
+        early = keep.tile([P, S], F32, name="early", tag="b_sb2", align_bytes=64)
+        late = keep.tile([P, 7 * CHUNK], F32, name="late", align_bytes=64)
+        u_high = [late[:, 3 * CHUNK :].rearrange("p (e j) -> p e j", e=2), early[:].rearrange("p (e j) -> p e j", e=2)]
 
         out_rows = out_0.rearrange("(p t) j -> p t j", t=PACK)
         out_words = out_1[0].rearrange("p n t -> p (n t)").bitcast(I32)
         o_s = keep.tile([P, S], U8, name="o_s", align_bytes=64)
-        u_low = keep.tile([P, 2, S], F32, name="u_low", align_bytes=64)
-        look_up(u_low[:, 0, :], b_sb[0], 0, S, scaled_low[:, 0, :], ALU.subtract)
-        look_up(u_low[:, 1, :], b_sb[1], 0, S, scaled_low[:, 1, :], ALU.subtract)
-        scaled2 = keep.tile([P, S], F32, name="scaled2")
-        look_up(scaled2[:], g_sb[2], 0, S, h_sb[2][:], ALU.mult)
-        scaled3 = keep.tile([P, HALF], F32, name="scaled3")
-        look_up(scaled3[:], g_sb[3], 0, HALF, h_sb[3][:, halves[0]], ALU.mult)
-        late = keep.tile([P, 7 * CHUNK], F32, name="late", align_bytes=64)
-        u_first = late[:, 3 * CHUNK :].rearrange("p (e j) -> p e j", e=2)
-        z_late = late[:, 0:S].bitcast(BF16).rearrange("p (j t) -> p j t", t=PACK)
-        early = keep.tile([P, S], F32, name="early", align_bytes=64)
-        u_second = early[:].rearrange("p (e j) -> p e j", e=2)
-        z_early = early[:].bitcast(BF16).rearrange("p (j t) -> p j t", t=PACK)
-        z_sb = [z[:, c * CHUNK : (c + 1) * CHUNK, :] for z in (z_early, z_late) for c in range(2)]
+        z_flat = [early[:].bitcast(BF16), late[:, 0:S].bitcast(BF16)]
+        z_sb = [z.rearrange("p (j t) -> p j t", t=PACK) for z in z_flat]
 
-        def add_shift(u, e, a):
-            scaled = scaled3[:] if e else scaled2[:, halves[a]]
-            look_up(u[:, e, :], b_sb[2 + e], a * HALF, HALF, scaled, ALU.add)
+        def gelu_low(a):
+            nc.scalar.activation(z_sb[a][:, :, 0:2], u_low[:, :, halves[a]].rearrange("p e j -> p j e"), ACT.Gelu_apprx_tanh)
 
-        def gelu(pair, c, u, first):
-            cols = slice(c * CHUNK - first, (c + 1) * CHUNK - first)
-            nc.scalar.activation(z_sb[c][:, :, 2 * pair : 2 * pair + 2], u[:, :, cols].rearrange("p e j -> p j e"), ACT.Gelu_apprx_tanh)
+        def gelu_high(c):
+            cols = slice(c % 2 * CHUNK, (c % 2 + 1) * CHUNK)
+            nc.scalar.activation(z_sb[c // 2][:, cols, 2:4], u_high[c // 2][:, :, cols].rearrange("p e j -> p j e"), ACT.Gelu_apprx_tanh)
+
+        def gain3(a):
+            look_up(prod3[:], g_sb[3], a, h_high[:, 1, halves[a]], ALU.mult)
+
+        def sums_high(a):
+            nc.vector.tensor_tensor(u_high[a][:, 0, :], prod[2][:, halves[a]], shift[2][:, halves[a]], ALU.add)
+            look_up(u_high[a][:, 1, :], b_sb[3], a, prod3[:], ALU.add)
 
         def second_product(c, bank_tags):
             z_w = keep.tile([P, CHUNK], U32, name="z_w%d" % c, align_bytes=64)
             z_s = keep.tile([P, CHUNK], U8, name="z_s%d" % c, align_bytes=64)
-            nc.vector.quantize_mx(out=z_w[:].bitcast(FP8X4), scales=z_s[:], in_=z_sb[c].rearrange("p j t -> p (j t)"))
+            first = c % 2 * CHUNK * PACK
+            nc.vector.quantize_mx(out=z_w[:].bitcast(FP8X4), scales=z_s[:], in_=z_flat[c // 2][:, first : first + CHUNK * PACK])
             per_bank = PACK // len(bank_tags)
             banks = [psum.tile([P, per_bank, CHUNK], F32, name="acc%d_%s" % (c, tag), tag=tag) for tag in bank_tags]
             for t in range(PACK):
@@ -242,7 +247,7 @@ def tile_picked_adain8_gelu_po_kernel(
             return banks
 
         o32 = [keep.tile([P, PACK, CHUNK], F32, name="o32_%d" % c) for c in range(S // CHUNK)]
-        o16 = [keep.tile([P, 2, CHUNK, PACK], BF16, name="o16_%d" % a, tag=tag, align_bytes=64) for a, tag in enumerate(("b_sb2", "o16_1"))]
+        o16 = [keep.tile([P, 2, CHUNK, PACK], BF16, name="o16_%d" % a, align_bytes=64) for a in range(2)]
         o_w = [keep.tile([P, HALF], U32, name="o_w%d" % a, align_bytes=64) for a in range(2)]
 
         def store(c):
@@ -258,27 +263,25 @@ def tile_picked_adain8_gelu_po_kernel(
                 in_=o16[a][:, first : first + count, :, :].rearrange("p c j t -> p (c j t)"),
             )
 
+        gain3(0)
+        gelu_low(0)
+        sums_high(0)
         for c in (0, 1):
-            gelu(0, c, u_low, 0)
-        for e in range(2):
-            add_shift(u_first, e, 0)
-        for c in (0, 1):
-            gelu(1, c, u_first, 0)
-        nc.scalar.activation(z_late[:, :, 0:2], u_low[:, :, halves[1]].rearrange("p e j -> p j e"), ACT.Gelu_apprx_tanh)
+            gelu_high(c)
+        gelu_low(1)
         w2_d = keep.tile([P, N], U32, name="w2_d", align_bytes=64)
         deal(w2_d, w2_w)
-        look_up(scaled3[:], g_sb[3], HALF, HALF, h_sb[3][:, halves[1]], ALU.mult)
-        acc0 = second_product(0, ["y1_0"])
-        acc1 = second_product(1, ["y1_1"])
-        for e in range(2):
-            add_shift(u_second, e, 1)
+        gain3(1)
+        acc0 = second_product(0, ["acc0"])
+        acc1 = second_product(1, ["acc1"])
+        sums_high(1)
         nc.scalar.copy(o32[0][:], acc0[0][:])
         store(0)
         for c in (2, 3):
-            gelu(1, c, u_second, HALF)
+            gelu_high(c)
         nc.vector.tensor_copy(o32[1][:], acc1[0][:])
         store(1)
-        acc2 = second_product(2, ["y2", "y3"])
+        acc2 = second_product(2, ["y1_0", "y1_1"])
         round_out(0)
         acc3 = second_product(3, ["y0_0", "y0_1"])
         round_out(1)

@@ -179,8 +179,7 @@ def tile_picked_adain8_gelu_po_kernel(
         nc.vector.bn_stats(stats[3][:], y_whole[3][:])
         aggregate(2)
 
-        prod = [plane("prod%d" % t) for t in range(3)]
-        prod3 = keep.tile([P, HALF], F32, name="prod3", align_bytes=64)
+        prod = [plane("prod%d" % t) for t in range(PACK)]
 
         def centre_and_gain(t, a):
             nc.vector.scalar_tensor_tensor(prod[t][:, halves[a]], y_half[t][a][:], mean_of(t), gain[t][:, halves[a]], ALU.subtract, ALU.mult)
@@ -207,35 +206,25 @@ def tile_picked_adain8_gelu_po_kernel(
             nc.scalar.activation(h_high[:, t - 2, :], y_whole[t][:], ACT.Identity, bias=offset[t][:], scale=rstd[t])
         shift.append(fetch("shift2", b_sb[2], "offset2"))
         nc.vector.tensor_tensor(prod[2][:], g_sb[2][:].indirect(sty_sb[:]), h_high[:, 0, :], ALU.mult)
-        early = keep.tile([P, S], F32, name="early", tag="b_sb2", align_bytes=64)
-        late = keep.tile([P, 7 * CHUNK], F32, name="late", align_bytes=64)
-        u_high = [late[:, 3 * CHUNK :].rearrange("p (e j) -> p e j", e=2), early[:].rearrange("p (e j) -> p e j", e=2)]
+        u_high = keep.tile([P, 2, S], F32, name="u_high", align_bytes=64)
+        nc.vector.tensor_tensor(prod[3][:], g_sb[3][:].indirect(sty_sb[:]), h_high[:, 1, :], ALU.mult)
+        nc.vector.tensor_tensor(u_high[:, 0, :], prod[2][:], shift[2][:], ALU.add)
 
         out_rows = out_0.rearrange("(p t) j -> p t j", t=PACK)
         out_words = out_1[0].rearrange("p n t -> p (n t)").bitcast(I32)
         o_s = keep.tile([P, S], U8, name="o_s", align_bytes=64)
-        z_flat = [early[:].bitcast(BF16), late[:, 0:S].bitcast(BF16)]
-        z_sb = [z.rearrange("p (j t) -> p j t", t=PACK) for z in z_flat]
-
-        def gelu_low(a):
-            nc.scalar.activation(z_sb[a][:, :, 0:2], u_low[:, :, halves[a]].rearrange("p e j -> p j e"), ACT.Gelu_apprx_tanh)
+        z_flat = keep.tile([P, S * PACK], BF16, name="z_flat", tag="b_sb2", align_bytes=64)
+        z_sb = z_flat[:].rearrange("p (j t) -> p j t", t=PACK)
 
         def gelu_high(c):
-            cols = slice(c % 2 * CHUNK, (c % 2 + 1) * CHUNK)
-            nc.scalar.activation(z_sb[c // 2][:, cols, 2:4], u_high[c // 2][:, :, cols].rearrange("p e j -> p j e"), ACT.Gelu_apprx_tanh)
-
-        def gain3(a):
-            look_up(prod3[:], g_sb[3], a, h_high[:, 1, halves[a]], ALU.mult)
-
-        def sums_high(a):
-            nc.vector.tensor_tensor(u_high[a][:, 0, :], prod[2][:, halves[a]], shift[2][:, halves[a]], ALU.add)
-            look_up(u_high[a][:, 1, :], b_sb[3], a, prod3[:], ALU.add)
+            cols = slice(c * CHUNK, (c + 1) * CHUNK)
+            nc.scalar.activation(z_sb[:, cols, 2:4], u_high[:, :, cols].rearrange("p e j -> p j e"), ACT.Gelu_apprx_tanh)
 
         def second_product(c, bank_tags):
             z_w = keep.tile([P, CHUNK], U32, name="z_w%d" % c, align_bytes=64)
             z_s = keep.tile([P, CHUNK], U8, name="z_s%d" % c, align_bytes=64)
-            first = c % 2 * CHUNK * PACK
-            nc.vector.quantize_mx(out=z_w[:].bitcast(FP8X4), scales=z_s[:], in_=z_flat[c // 2][:, first : first + CHUNK * PACK])
+            first = c * CHUNK * PACK
+            nc.vector.quantize_mx(out=z_w[:].bitcast(FP8X4), scales=z_s[:], in_=z_flat[:, first : first + CHUNK * PACK])
             per_bank = PACK // len(bank_tags)
             banks = [psum.tile([P, per_bank, CHUNK], F32, name="acc%d_%s" % (c, tag), tag=tag) for tag in bank_tags]
             for t in range(PACK):
@@ -263,36 +252,31 @@ def tile_picked_adain8_gelu_po_kernel(
                 in_=o16[a][:, first : first + count, :, :].rearrange("p c j t -> p (c j t)"),
             )
 
-        gain3(0)
-        gelu_low(0)
-        sums_high(0)
-        for c in (0, 1):
+        nc.scalar.activation(z_sb[:, :, 0:2], u_low[:].rearrange("p e j -> p j e"), ACT.Gelu_apprx_tanh)
+        for a in range(2):
+            look_up(u_high[:, 1, halves[a]], b_sb[3], a, prod[3][:, halves[a]], ALU.add)
+        for c in range(S // CHUNK):
             gelu_high(c)
-        gelu_low(1)
         w2_d = keep.tile([P, N], U32, name="w2_d", align_bytes=64)
         deal(w2_d, w2_w)
-        gain3(1)
         acc0 = second_product(0, ["acc0"])
         acc1 = second_product(1, ["acc1"])
-        sums_high(1)
         nc.scalar.copy(o32[0][:], acc0[0][:])
         store(0)
-        for c in (2, 3):
-            gelu_high(c)
+        acc2 = second_product(2, ["y1_0", "y1_1"])
+        acc3 = second_product(3, ["y0_0", "y0_1"])
         nc.vector.tensor_copy(o32[1][:], acc1[0][:])
         store(1)
-        acc2 = second_product(2, ["y1_0", "y1_1"])
         round_out(0)
-        acc3 = second_product(3, ["y0_0", "y0_1"])
         round_out(1)
-        quantise_out(0, 0, 2)
-        nc.sync.dma_start(out=out_words[:, halves[0]], in_=o_w[0][:].bitcast(I32))
         nc.scalar.copy(o32[2][:, 0:2, :], acc2[0][:])
         nc.scalar.copy(o32[2][:, 2:4, :], acc2[1][:])
         store(2)
-        nc.vector.tensor_copy(o32[3][:, 0:2, :], acc3[0][:])
+        nc.scalar.copy(o32[3][:, 0:2, :], acc3[0][:])
         nc.scalar.copy(o32[3][:, 2:4, :], acc3[1][:])
         store(3)
+        quantise_out(0, 0, 2)
+        nc.sync.dma_start(out=out_words[:, halves[0]], in_=o_w[0][:].bitcast(I32))
         round_out(2)
         round_out(3)
         quantise_out(1, 0, 1)

@@ -49,11 +49,12 @@ def tile_picked_adain8_gelu_po_kernel(
         g_sb = [keep.tile([P, U], F32, name="g_sb%d" % t, tag="g_sb%d" % t) for t in range(PACK)]
         b_sb = [keep.tile([P, U], F32, name="b_sb%d" % t, tag="b_sb%d" % t, align_bytes=64) for t in range(PACK)]
 
-        for scale_tile in (x_s, w1_s, w2_s):
+        nc.gpsimd.memset(x_s[:].bitcast(I32), 0)
+        for scale_tile in (w1_s, w2_s):
             nc.vector.memset(scale_tile[:].bitcast(I32), 0)
 
         one = keep.tile([P, 2], F32, name="one", align_bytes=64)
-        nc.vector.memset(one[:], 1.0)
+        nc.gpsimd.memset(one[:], 1.0)
         power = keep.tile([P, 2], F32, name="power", align_bytes=64)
         nc.gpsimd.tensor_scalar(power[:], one[:], -0.5, None, ALU.mult)
 
@@ -88,9 +89,10 @@ def tile_picked_adain8_gelu_po_kernel(
         xg_s = keep.tile([P, S], U8, name="xg_s", align_bytes=64)
         w1_d = keep.tile([P, H], U32, name="w1_d", align_bytes=64)
 
-        def deal(dst, src):
+        def deal(dst, src, planes):
             nc.vector.tensor_copy(
-                out=dst[:].rearrange("p (t m) -> p m t", t=PACK), in_=src[:].rearrange("p (m t) -> p m t", t=PACK)
+                out=dst[:].rearrange("p (t m) -> p m t", t=PACK)[:, :, planes],
+                in_=src[:].rearrange("p (m t) -> p m t", t=PACK)[:, :, planes],
             )
 
         def deal_bytes(dst, src, planes):
@@ -102,7 +104,7 @@ def tile_picked_adain8_gelu_po_kernel(
         halves = [slice(0, HALF), slice(HALF, S)]
         half_lists = [slice(0, HALF // GROUP), slice(HALF // GROUP, S // GROUP)]
 
-        deal(w1_d, w1_w)
+        deal(w1_d, w1_w, slice(0, 4))
         nc.vector.tensor_copy(xg_s[:], x_s[:].indirect(offs_sb[:]))
         xg_w = [keep.tile([P, HALF], U32, name="xg_w%d" % a, align_bytes=64) for a in range(2)]
         for a in range(2):
@@ -133,8 +135,8 @@ def tile_picked_adain8_gelu_po_kernel(
         def columns(name, count):
             return keep.tile([P, count], F32, name=name, tag=name, align_bytes=64)
 
-        def fetch(name, table, tag=None):
-            picked = keep.tile([P, S], F32, name=name, tag=tag or name, align_bytes=64)
+        def fetch(name, table):
+            picked = keep.tile([P, S], F32, name=name, align_bytes=64)
             nc.scalar.activation(picked[:], table[:].indirect(sty_sb[:]), ACT.Copy)
             return picked
 
@@ -166,6 +168,7 @@ def tile_picked_adain8_gelu_po_kernel(
             nc.gpsimd.tensor_tensor(both[:], spread[:], power[:], ALU.pow)
             for i, t in enumerate(pairs[e]):
                 rstd[t] = both[:, i : i + 1]
+            return both
 
         w2s_d = keep.tile([P, N], U8, name="w2s_d", align_bytes=64)
         deal_bytes(w2s_d, w2_s, slice(0, 4))
@@ -184,15 +187,13 @@ def tile_picked_adain8_gelu_po_kernel(
         def centre_and_gain(t, a):
             nc.vector.scalar_tensor_tensor(prod[t][:, halves[a]], y_half[t][a][:], mean_of(t), gain[t][:, halves[a]], ALU.subtract, ALU.mult)
 
-        centre_and_gain(0, 0)
         aggregate(3)
-        rstd_of(1)
-        offset = {t: columns("offset%d" % t, 1) for t in (2, 3)}
-        for t in (2, 3):
-            nc.gpsimd.tensor_scalar(offset[t][:], mean_of(t), rstd[t], -1.0, ALU.mult, ALU.mult)
-        centre_and_gain(0, 1)
-        for a in range(2):
-            centre_and_gain(1, a)
+        rstd_high = rstd_of(1)
+        for t in range(2):
+            for a in range(2):
+                centre_and_gain(t, a)
+        offset = columns("offset", 2)
+        nc.vector.scalar_tensor_tensor(offset[:], moments[1][:, :, 0], -1.0, rstd_high[:], ALU.mult, ALU.mult)
 
         u_low = keep.tile([P, 2, S], F32, name="u_low", align_bytes=64)
 
@@ -203,8 +204,8 @@ def tile_picked_adain8_gelu_po_kernel(
             scale_and_shift(u_low[:, t, :], t, slice(0, S))
         h_high = keep.tile([P, 2, S], F32, name="h_high", tag="b_sb1", align_bytes=64)
         for t in (2, 3):
-            nc.scalar.activation(h_high[:, t - 2, :], y_whole[t][:], ACT.Identity, bias=offset[t][:], scale=rstd[t])
-        shift.append(fetch("shift2", b_sb[2], "offset2"))
+            nc.scalar.activation(h_high[:, t - 2, :], y_whole[t][:], ACT.Identity, bias=offset[:, t - 2 : t - 1], scale=rstd[t])
+        shift.append(fetch("shift2", b_sb[2]))
         nc.vector.tensor_tensor(prod[2][:], g_sb[2][:].indirect(sty_sb[:]), h_high[:, 0, :], ALU.mult)
         u_high = keep.tile([P, 2, S], F32, name="u_high", align_bytes=64)
         nc.vector.tensor_tensor(prod[3][:], g_sb[3][:].indirect(sty_sb[:]), h_high[:, 1, :], ALU.mult)
@@ -221,10 +222,12 @@ def tile_picked_adain8_gelu_po_kernel(
             nc.scalar.activation(z_sb[:, cols, 2:4], u_high[:, :, cols].rearrange("p e j -> p j e"), ACT.Gelu_apprx_tanh)
 
         def second_product(c, bank_tags):
-            z_w = keep.tile([P, CHUNK], U32, name="z_w%d" % c, align_bytes=64)
+            z_w = keep.tile([P, CHUNK], U32, name="z_w%d" % c, tag="z_w%d" % (c % 3), align_bytes=64)
             z_s = keep.tile([P, CHUNK], U8, name="z_s%d" % c, align_bytes=64)
             first = c * CHUNK * PACK
             nc.vector.quantize_mx(out=z_w[:].bitcast(FP8X4), scales=z_s[:], in_=z_flat[:, first : first + CHUNK * PACK])
+            if c == 0:
+                deal(w2_d, w2_w, slice(2, 4))
             per_bank = PACK // len(bank_tags)
             banks = [psum.tile([P, per_bank, CHUNK], F32, name="acc%d_%s" % (c, tag), tag=tag) for tag in bank_tags]
             for t in range(PACK):
@@ -235,54 +238,53 @@ def tile_picked_adain8_gelu_po_kernel(
                 )
             return banks
 
-        o32 = [keep.tile([P, PACK, CHUNK], F32, name="o32_%d" % c) for c in range(S // CHUNK)]
+        o32 = [keep.tile([P, PACK, CHUNK], F32, name="o32_%d" % c)[:] for c in range(2)]
+        o32_second = keep.tile([P, PACK, HALF], F32, name="o32_second")
+        o32.extend(o32_second[:, :, c * CHUNK : (c + 1) * CHUNK] for c in range(2))
         o16 = [keep.tile([P, 2, CHUNK, PACK], BF16, name="o16_%d" % a, align_bytes=64) for a in range(2)]
-        o_w = [keep.tile([P, HALF], U32, name="o_w%d" % a, align_bytes=64) for a in range(2)]
-
-        def store(c):
-            nc.sync.dma_start(out=out_rows[:, :, c * CHUNK : (c + 1) * CHUNK], in_=o32[c][:])
+        o_w = keep.tile([P, S], U32, name="o_w", align_bytes=64)
 
         def round_out(c):
-            nc.vector.tensor_copy(o16[c // 2][:, c % 2, :, :], o32[c][:].rearrange("p t j -> p j t"))
+            nc.vector.tensor_copy(o16[c // 2][:, c % 2, :, :], o32[c].rearrange("p t j -> p j t"))
 
         def quantise_out(a, first, count):
-            cols = slice(first * CHUNK, (first + count) * CHUNK)
+            cols = slice(a * HALF + first * CHUNK, a * HALF + (first + count) * CHUNK)
             nc.vector.quantize_mx(
-                out=o_w[a][:, cols].bitcast(FP8X4), scales=o_s[:, a * HALF + first * CHUNK : a * HALF + (first + count) * CHUNK],
+                out=o_w[:, cols].bitcast(FP8X4), scales=o_s[:, cols],
                 in_=o16[a][:, first : first + count, :, :].rearrange("p c j t -> p (c j t)"),
             )
 
         nc.scalar.activation(z_sb[:, :, 0:2], u_low[:].rearrange("p e j -> p j e"), ACT.Gelu_apprx_tanh)
-        for a in range(2):
-            look_up(u_high[:, 1, halves[a]], b_sb[3], a, prod[3][:, halves[a]], ALU.add)
+        look_up(u_high[:, 1, halves[0]], b_sb[3], 0, prod[3][:, halves[0]], ALU.add)
+        shift3 = keep.tile([P, HALF], F32, name="shift3", align_bytes=64)
+        nc.scalar.activation(shift3[:], b_sb[3][:].indirect(sty_sb[:, half_lists[1]]), ACT.Copy)
+        w2_d = keep.tile([P, N], U32, name="w2_d", align_bytes=64)
+        deal(w2_d, w2_w, slice(0, 2))
+        nc.vector.tensor_tensor(u_high[:, 1, halves[1]], prod[3][:, halves[1]], shift3[:], ALU.add)
         for c in range(S // CHUNK):
             gelu_high(c)
-        w2_d = keep.tile([P, N], U32, name="w2_d", align_bytes=64)
-        deal(w2_d, w2_w)
-        acc0 = second_product(0, ["acc0"])
-        acc1 = second_product(1, ["acc1"])
-        nc.scalar.copy(o32[0][:], acc0[0][:])
-        store(0)
-        acc2 = second_product(2, ["y1_0", "y1_1"])
-        acc3 = second_product(3, ["y0_0", "y0_1"])
-        nc.vector.tensor_copy(o32[1][:], acc1[0][:])
-        store(1)
-        round_out(0)
-        round_out(1)
-        nc.scalar.copy(o32[2][:, 0:2, :], acc2[0][:])
-        nc.scalar.copy(o32[2][:, 2:4, :], acc2[1][:])
-        store(2)
-        nc.scalar.copy(o32[3][:, 0:2, :], acc3[0][:])
-        nc.scalar.copy(o32[3][:, 2:4, :], acc3[1][:])
-        store(3)
+        acc0 = second_product(0, ["acc0", "acc1"])
+        acc1 = second_product(1, ["y2"])
+        acc2 = second_product(2, ["y0_0", "y0_1"])
+        nc.vector.tensor_copy(o32[0][:, 0:2, :], acc0[0][:])
+        nc.sync.dma_start(out=out_rows[:, 0:2, 0:CHUNK], in_=o32[0][:, 0:2, :])
+        nc.scalar.copy(o32[0][:, 2:4, :], acc0[1][:])
+        nc.sync.dma_start(out=out_rows[:, 2:4, 0:CHUNK], in_=o32[0][:, 2:4, :])
+        acc3 = second_product(3, ["y1_0", "y1_1"])
+        nc.vector.tensor_copy(o32[1], acc1[0][:])
+        nc.sync.dma_start(out=out_rows[:, :, CHUNK:HALF], in_=o32[1])
+        for c, acc in ((2, acc2), (3, acc3)):
+            for e in range(2):
+                nc.scalar.copy(o32[c][:, 2 * e : 2 * e + 2, :], acc[e][:])
+        nc.sync.dma_start(out=out_rows[:, :, halves[1]], in_=o32_second[:])
+        for c in range(3):
+            round_out(c)
         quantise_out(0, 0, 2)
-        nc.sync.dma_start(out=out_words[:, halves[0]], in_=o_w[0][:].bitcast(I32))
-        round_out(2)
         round_out(3)
         quantise_out(1, 0, 1)
         quantise_out(1, 1, 1)
 
-        nc.scalar.dma_start(out=out_words[:, halves[1]], in_=o_w[1][:].bitcast(I32))
+        nc.scalar.dma_start(out=out_words, in_=o_w[:].bitcast(I32))
         for r in range(PACK):
             eng = nc.scalar if r % 2 else nc.sync
             eng.dma_start(out=out_2[0, r:SCALE_ROWS:PACK, :].bitcast(I32), in_=o_s[r:P:QUADRANT, :].bitcast(I32))

@@ -195,21 +195,20 @@ def tile_picked_adain8_gelu_po_kernel(
         offset = columns("offset", 2)
         nc.vector.scalar_tensor_tensor(offset[:], moments[1][:, :, 0], -1.0, rstd_high[:], ALU.mult, ALU.mult)
 
-        u_low = keep.tile([P, 2, S], F32, name="u_low", align_bytes=64)
+        u = keep.tile([P, PACK, S], F32, name="u", align_bytes=64)
 
         def scale_and_shift(out, t, cols):
             nc.vector.scalar_tensor_tensor(out, prod[t][:, cols], rstd[t], shift[t][:, cols], ALU.mult, ALU.add)
 
         for t in range(2):
-            scale_and_shift(u_low[:, t, :], t, slice(0, S))
+            scale_and_shift(u[:, t, :], t, slice(0, S))
         h_high = keep.tile([P, 2, S], F32, name="h_high", tag="b_sb1", align_bytes=64)
         for t in (2, 3):
             nc.scalar.activation(h_high[:, t - 2, :], y_whole[t][:], ACT.Identity, bias=offset[:, t - 2 : t - 1], scale=rstd[t])
         shift.append(fetch("shift2", b_sb[2]))
         nc.vector.tensor_tensor(prod[2][:], g_sb[2][:].indirect(sty_sb[:]), h_high[:, 0, :], ALU.mult)
-        u_high = keep.tile([P, 2, S], F32, name="u_high", align_bytes=64)
         nc.vector.tensor_tensor(prod[3][:], g_sb[3][:].indirect(sty_sb[:]), h_high[:, 1, :], ALU.mult)
-        nc.vector.tensor_tensor(u_high[:, 0, :], prod[2][:], shift[2][:], ALU.add)
+        nc.vector.tensor_tensor(u[:, 2, :], prod[2][:], shift[2][:], ALU.add)
 
         out_rows = out_0.rearrange("(p t) j -> p t j", t=PACK)
         out_words = out_1[0].rearrange("p n t -> p (n t)").bitcast(I32)
@@ -217,13 +216,13 @@ def tile_picked_adain8_gelu_po_kernel(
         z_flat = keep.tile([P, S * PACK], BF16, name="z_flat", tag="b_sb2", align_bytes=64)
         z_sb = z_flat[:].rearrange("p (j t) -> p j t", t=PACK)
 
-        def gelu_high(c):
-            cols = slice(c * CHUNK, (c + 1) * CHUNK)
-            nc.scalar.activation(z_sb[:, cols, 2:4], u_high[:, :, cols].rearrange("p e j -> p j e"), ACT.Gelu_apprx_tanh)
+        def gelu(planes, first, last):
+            cols = slice(first * CHUNK, last * CHUNK)
+            nc.scalar.activation(z_sb[:, cols, planes], u[:, planes, cols].rearrange("p t j -> p j t"), ACT.Gelu_apprx_tanh)
 
         def second_product(c, bank_tags):
-            z_w = keep.tile([P, CHUNK], U32, name="z_w%d" % c, tag="z_w%d" % (c % 3), align_bytes=64)
-            z_s = keep.tile([P, CHUNK], U8, name="z_s%d" % c, align_bytes=64)
+            z_w = keep.tile([P, CHUNK], U32, name="z_w%d" % c, tag="z_w%d" % (0, 1, 0, 3)[c], align_bytes=64)
+            z_s = keep.tile([P, CHUNK], U8, name="z_s%d" % c, tag="z_s%d" % (c % 3), align_bytes=64)
             first = c * CHUNK * PACK
             nc.vector.quantize_mx(out=z_w[:].bitcast(FP8X4), scales=z_s[:], in_=z_flat[:, first : first + CHUNK * PACK])
             if c == 0:
@@ -254,37 +253,41 @@ def tile_picked_adain8_gelu_po_kernel(
                 in_=o16[a][:, first : first + count, :, :].rearrange("p c j t -> p (c j t)"),
             )
 
-        nc.scalar.activation(z_sb[:, :, 0:2], u_low[:].rearrange("p e j -> p j e"), ACT.Gelu_apprx_tanh)
-        look_up(u_high[:, 1, halves[0]], b_sb[3], 0, prod[3][:, halves[0]], ALU.add)
+        gelu(slice(0, 2), 0, 3)
+        look_up(u[:, 3, halves[0]], b_sb[3], 0, prod[3][:, halves[0]], ALU.add)
         shift3 = keep.tile([P, HALF], F32, name="shift3", align_bytes=64)
         nc.scalar.activation(shift3[:], b_sb[3][:].indirect(sty_sb[:, half_lists[1]]), ACT.Copy)
         w2_d = keep.tile([P, N], U32, name="w2_d", align_bytes=64)
         deal(w2_d, w2_w, slice(0, 2))
-        nc.vector.tensor_tensor(u_high[:, 1, halves[1]], prod[3][:, halves[1]], shift3[:], ALU.add)
-        for c in range(S // CHUNK):
-            gelu_high(c)
+        nc.vector.tensor_tensor(u[:, 3, halves[1]], prod[3][:, halves[1]], shift3[:], ALU.add)
+        for c in range(3):
+            gelu(slice(2, 4), c, c + 1)
+        gelu(slice(0, 4), 3, 4)
         acc0 = second_product(0, ["acc0", "acc1"])
         acc1 = second_product(1, ["y2"])
-        acc2 = second_product(2, ["y0_0", "y0_1"])
         nc.vector.tensor_copy(o32[0][:, 0:2, :], acc0[0][:])
         nc.sync.dma_start(out=out_rows[:, 0:2, 0:CHUNK], in_=o32[0][:, 0:2, :])
-        nc.scalar.copy(o32[0][:, 2:4, :], acc0[1][:])
+        acc2 = second_product(2, ["y0_0", "y0_1"])
+        nc.vector.tensor_copy(o32[0][:, 2:4, :], acc0[1][:])
         nc.sync.dma_start(out=out_rows[:, 2:4, 0:CHUNK], in_=o32[0][:, 2:4, :])
         acc3 = second_product(3, ["y1_0", "y1_1"])
-        nc.vector.tensor_copy(o32[1], acc1[0][:])
+        nc.scalar.copy(o32[1], acc1[0][:])
         nc.sync.dma_start(out=out_rows[:, :, CHUNK:HALF], in_=o32[1])
         for c, acc in ((2, acc2), (3, acc3)):
             for e in range(2):
                 nc.scalar.copy(o32[c][:, 2 * e : 2 * e + 2, :], acc[e][:])
-        nc.sync.dma_start(out=out_rows[:, :, halves[1]], in_=o32_second[:])
-        for c in range(3):
+        for c in range(2):
             round_out(c)
-        quantise_out(0, 0, 2)
+        quantise_out(0, 0, 1)
+        quantise_out(0, 1, 1)
+        nc.sync.dma_start(out=out_words[:, halves[0]], in_=o_w[:, halves[0]].bitcast(I32))
+        nc.sync.dma_start(out=out_rows[:, :, halves[1]], in_=o32_second[:])
+        round_out(2)
         round_out(3)
         quantise_out(1, 0, 1)
         quantise_out(1, 1, 1)
 
-        nc.scalar.dma_start(out=out_words, in_=o_w[:].bitcast(I32))
+        nc.scalar.dma_start(out=out_words[:, halves[1]], in_=o_w[:, halves[1]].bitcast(I32))
         for r in range(PACK):
             eng = nc.scalar if r % 2 else nc.sync
             eng.dma_start(out=out_2[0, r:SCALE_ROWS:PACK, :].bitcast(I32), in_=o_s[r:P:QUADRANT, :].bitcast(I32))

@@ -161,14 +161,13 @@ def tile_picked_adain8_gelu_po_kernel(
             src = stats[t][:].rearrange("p a s -> p (a s)") if t in y_half else stats[t][:]
             nc.vector.bn_aggr(moment_of[t], src)
 
-        def rstd_of(e):
-            spread = keep.tile([P, 2], F32, name="spread%d" % e, tag="spread0", align_bytes=64)
-            nc.gpsimd.tensor_scalar(spread[:], moments[e][:, :, 1], EPS, None, ALU.add)
-            both = columns("rstd%d" % e, 2)
+        def rstd_of(e, engine, spread_tag, rstd_tag):
+            spread = keep.tile([P, 2], F32, name="spread%d" % e, tag=spread_tag, align_bytes=64)
+            engine.tensor_scalar(spread[:], moments[e][:, :, 1], EPS, None, ALU.add)
+            both = keep.tile([P, 2], F32, name="rstd%d" % e, tag=rstd_tag, align_bytes=64)
             nc.gpsimd.tensor_tensor(both[:], spread[:], power[:], ALU.pow)
             for i, t in enumerate(pairs[e]):
                 rstd[t] = both[:, i : i + 1]
-            return both
 
         w2s_d = keep.tile([P, N], U8, name="w2s_d", align_bytes=64)
         deal_bytes(w2s_d, w2_s, slice(0, 4))
@@ -178,7 +177,7 @@ def tile_picked_adain8_gelu_po_kernel(
         aggregate(0)
         nc.vector.bn_stats(stats[2][:], y_whole[2][:])
         aggregate(1)
-        rstd_of(0)
+        rstd_of(0, nc.gpsimd, "spread0", "rstd0")
         nc.vector.bn_stats(stats[3][:], y_whole[3][:])
         aggregate(2)
 
@@ -188,27 +187,30 @@ def tile_picked_adain8_gelu_po_kernel(
             nc.vector.scalar_tensor_tensor(prod[t][:, halves[a]], y_half[t][a][:], mean_of(t), gain[t][:, halves[a]], ALU.subtract, ALU.mult)
 
         aggregate(3)
-        rstd_high = rstd_of(1)
-        for t in range(2):
-            for a in range(2):
-                centre_and_gain(t, a)
-        offset = columns("offset", 2)
-        nc.vector.scalar_tensor_tensor(offset[:], moments[1][:, :, 0], -1.0, rstd_high[:], ALU.mult, ALU.mult)
+        centre_and_gain(0, 0)
+        rstd_of(1, nc.vector, "spread1", "spread0")
+        centre_and_gain(0, 1)
+        for a in range(2):
+            centre_and_gain(1, a)
 
-        u = keep.tile([P, PACK, S], F32, name="u", align_bytes=64)
+        u = keep.tile([P, PACK, S], F32, name="u", tag="u", align_bytes=64)
 
         def scale_and_shift(out, t, cols):
             nc.vector.scalar_tensor_tensor(out, prod[t][:, cols], rstd[t], shift[t][:, cols], ALU.mult, ALU.add)
 
-        for t in range(2):
-            scale_and_shift(u[:, t, :], t, slice(0, S))
+        scale_and_shift(u[:, 0, :], 0, slice(0, S))
+        late_columns = keep.tile([P, 2], F32, name="late_columns", tag="b_sb0", align_bytes=64)
+        offset3, neg_rstd2 = late_columns[:, 0:1], late_columns[:, 1:2]
+        nc.vector.tensor_scalar(offset3, mean_of(3), rstd[3], -1.0, ALU.mult, ALU.mult)
+        nc.vector.tensor_scalar(neg_rstd2, rstd[2], -1.0, None, ALU.mult)
+        scale_and_shift(u[:, 1, :], 1, slice(0, S))
         h_high = keep.tile([P, 2, S], F32, name="h_high", tag="b_sb1", align_bytes=64)
-        for t in (2, 3):
-            nc.scalar.activation(h_high[:, t - 2, :], y_whole[t][:], ACT.Identity, bias=offset[:, t - 2 : t - 1], scale=rstd[t])
+        nc.scalar.activation(h_high[:, 0, :], y_whole[2][:], ACT.Identity, bias=mean_of(2), scale=-1.0)
+        nc.scalar.activation(h_high[:, 1, :], y_whole[3][:], ACT.Identity, bias=offset3, scale=rstd[3])
         shift.append(fetch("shift2", b_sb[2]))
         nc.vector.tensor_tensor(prod[2][:], g_sb[2][:].indirect(sty_sb[:]), h_high[:, 0, :], ALU.mult)
         nc.vector.tensor_tensor(prod[3][:], g_sb[3][:].indirect(sty_sb[:]), h_high[:, 1, :], ALU.mult)
-        nc.vector.tensor_tensor(u[:, 2, :], prod[2][:], shift[2][:], ALU.add)
+        nc.vector.scalar_tensor_tensor(u[:, 2, :], prod[2][:], neg_rstd2, shift[2][:], ALU.mult, ALU.add)
 
         out_rows = out_0.rearrange("(p t) j -> p t j", t=PACK)
         out_words = out_1[0].rearrange("p n t -> p (n t)").bitcast(I32)
@@ -237,10 +239,10 @@ def tile_picked_adain8_gelu_po_kernel(
                 )
             return banks
 
-        o32 = [keep.tile([P, PACK, CHUNK], F32, name="o32_%d" % c)[:] for c in range(2)]
+        o32 = [keep.tile([P, PACK, CHUNK], F32, name="o32_%d" % c, tag=tag, align_bytes=64)[:] for c, tag in enumerate(("o32_0", "u"))]
         o32_second = keep.tile([P, PACK, HALF], F32, name="o32_second")
         o32.extend(o32_second[:, :, c * CHUNK : (c + 1) * CHUNK] for c in range(2))
-        o16 = [keep.tile([P, 2, CHUNK, PACK], BF16, name="o16_%d" % a, align_bytes=64) for a in range(2)]
+        o16 = [keep.tile([P, 2, CHUNK, PACK], BF16, name="o16_%d" % a, tag=tag, align_bytes=64) for a, tag in enumerate(("b_sb2", "o16_1"))]
         o_w = keep.tile([P, S], U32, name="o_w", align_bytes=64)
 
         def round_out(c):
@@ -264,30 +266,31 @@ def tile_picked_adain8_gelu_po_kernel(
             gelu(slice(2, 4), c, c + 1)
         gelu(slice(0, 4), 3, 4)
         acc0 = second_product(0, ["acc0", "acc1"])
-        acc1 = second_product(1, ["y2"])
+        acc1 = second_product(1, ["y2", "y3"])
         nc.vector.tensor_copy(o32[0][:, 0:2, :], acc0[0][:])
         nc.sync.dma_start(out=out_rows[:, 0:2, 0:CHUNK], in_=o32[0][:, 0:2, :])
         acc2 = second_product(2, ["y0_0", "y0_1"])
         nc.vector.tensor_copy(o32[0][:, 2:4, :], acc0[1][:])
         nc.sync.dma_start(out=out_rows[:, 2:4, 0:CHUNK], in_=o32[0][:, 2:4, :])
         acc3 = second_product(3, ["y1_0", "y1_1"])
-        nc.scalar.copy(o32[1], acc1[0][:])
+        nc.scalar.copy(o32[1][:, 0:2, :], acc1[0][:])
+        nc.vector.tensor_copy(o32[1][:, 2:4, :], acc1[1][:])
         nc.sync.dma_start(out=out_rows[:, :, CHUNK:HALF], in_=o32[1])
-        for c, acc in ((2, acc2), (3, acc3)):
-            for e in range(2):
-                nc.scalar.copy(o32[c][:, 2 * e : 2 * e + 2, :], acc[e][:])
+        for e in range(2):
+            nc.scalar.copy(o32[2][:, 2 * e : 2 * e + 2, :], acc2[e][:])
+        for e in range(2):
+            nc.scalar.copy(o32[3][:, 2 * e : 2 * e + 2, :], acc3[e][:])
+            nc.sync.dma_start(out=out_rows[:, 2 * e : 2 * e + 2, halves[1]], in_=o32_second[:, 2 * e : 2 * e + 2, :])
         for c in range(2):
             round_out(c)
         quantise_out(0, 0, 1)
         quantise_out(0, 1, 1)
-        nc.sync.dma_start(out=out_words[:, halves[0]], in_=o_w[:, halves[0]].bitcast(I32))
-        nc.sync.dma_start(out=out_rows[:, :, halves[1]], in_=o32_second[:])
         round_out(2)
         round_out(3)
         quantise_out(1, 0, 1)
         quantise_out(1, 1, 1)
 
-        nc.scalar.dma_start(out=out_words[:, halves[1]], in_=o_w[:, halves[1]].bitcast(I32))
+        nc.scalar.dma_start(out=out_words, in_=o_w[:].bitcast(I32))
         for r in range(PACK):
             eng = nc.scalar if r % 2 else nc.sync
             eng.dma_start(out=out_2[0, r:SCALE_ROWS:PACK, :].bitcast(I32), in_=o_s[r:P:QUADRANT, :].bitcast(I32))

from contextlib import ExitStack

import concourse.mybir as mybir

K, T, S, H, N, U = 512, 2048, 512, 512, 512, 1024
FLOPS = 2 * K * H * S + 2 * H * N * S

F32 = mybir.dt.float32
BF16 = mybir.dt.bfloat16
I32 = mybir.dt.int32
U32 = mybir.dt.uint32
U16 = mybir.dt.uint16
U8 = mybir.dt.uint8
FP8X4 = mybir.dt.float8_e4m3fn_x4
ACT = mybir.ActivationFunctionType
ALU = mybir.AluOpType

P = 128
PACK = 4
GROUP = 16
QUADRANT = 32
SCALE_ROWS = 16
HALF = 256
CHUNK = 128
W1_ROW, W2_ROW = 4, 8
EPS = 1e-5


def tile_picked_adain8_gelu_po_kernel(
    tc, x_words, x_scales, w1_words, w1_scales, gamma, beta, w2_words, w2_scales, offs, sty, out_0, out_1, out_2
):
    nc = tc.nc

    def words_of(dram):
        return dram[0].rearrange("p n t -> p (n t)").bitcast(I32)

    with ExitStack() as ctx:
        keep = ctx.enter_context(tc.tile_pool(name="keep", bufs=1))
        psum = ctx.enter_context(tc.psum_pool(name="psum", bufs=1))

        offs_sb = keep.tile([P, S // GROUP], U16, name="offs_sb")
        sty_sb = keep.tile([P, S // GROUP], U16, name="sty_sb")
        x_w = keep.tile([P, T], U32, name="x_w", tag="x_w", align_bytes=64)
        x_s = keep.tile([P, T], U8, name="x_s", align_bytes=64)
        w2_s = keep.tile([P, N], U8, name="w2_s", tag="spread0", align_bytes=64)
        w1_w = keep.tile([P, H], U32, name="w1_w", align_bytes=64)
        w2_w = keep.tile([P, N], U32, name="w2_w", align_bytes=64)
        w1_s = keep.tile([P, H], U8, name="w1_s", tag="w1_s", align_bytes=64)
        g_sb = [keep.tile([P, U], F32, name="g_sb%d" % t, tag="g_sb%d" % t) for t in range(PACK)]
        b_sb = [keep.tile([P, U], F32, name="b_sb%d" % t, tag="b_sb%d" % t, align_bytes=64) for t in range(PACK)]

        nc.gpsimd.memset(x_s[:].bitcast(I32), 0)
        for scale_tile in (w1_s, w2_s):
            nc.vector.memset(scale_tile[:].bitcast(I32), 0)

        one = keep.tile([P, 2], F32, name="one", align_bytes=64)
        nc.gpsimd.memset(one[:], 1.0)
        power = keep.tile([P, 2], F32, name="power", align_bytes=64)
        nc.gpsimd.tensor_scalar(power[:], one[:], -0.5, None, ALU.mult)

        g_rows = gamma.rearrange("(p t) u -> p t u", t=PACK)
        b_rows = beta.rearrange("(p t) u -> p t u", t=PACK)

        def load_scales(engines, tile, dram, first):
            for r in range(PACK):
                engines[r].dma_start(
                    out=tile[first + r : P : QUADRANT, :].bitcast(I32), in_=dram[0, r:SCALE_ROWS:PACK, :].bitcast(I32)
                )

        nc.sync.dma_start(offs_sb[:], offs)
        nc.sync.dma_start(out=w1_w[:].bitcast(I32), in_=words_of(w1_words))
        load_scales([nc.scalar, nc.scalar, nc.sync, nc.sync], x_s, x_scales, 0)
        nc.sync.dma_start(out=x_w[:].bitcast(I32), in_=words_of(x_words))
        unread = keep.tile([P, 1], F32, name="unread", align_bytes=64)
        nc.scalar.activation(unread[:], one[:, 0:1], ACT.Gelu_apprx_tanh)
        load_scales([nc.sync] * PACK, w1_s, w1_scales, W1_ROW)
        nc.sync.dma_start(sty_sb[:], sty)
        for t in (0, 1):
            nc.sync.dma_start(out=g_sb[t][:], in_=g_rows[:, t, :])
        load_scales([nc.sync] * PACK, w2_s, w2_scales, W2_ROW)
        for t in (0, 1):
            nc.sync.dma_start(out=b_sb[t][:], in_=b_rows[:, t, :])
        for t in (2, 3):
            nc.sync.dma_start(out=g_sb[t][:], in_=g_rows[:, t, :])
        for t in (2, 3):
            nc.sync.dma_start(out=b_sb[t][:], in_=b_rows[:, t, :])
        nc.sync.dma_start(out=w2_w[:].bitcast(I32), in_=words_of(w2_words))

        xg_s = keep.tile([P, S], U8, name="xg_s", align_bytes=64)
        w1_d = keep.tile([P, H], U32, name="w1_d", align_bytes=64)

        def deal(dst, src, planes):
            nc.vector.tensor_copy(
                out=dst[:].rearrange("p (t m) -> p m t", t=PACK)[:, :, planes],
                in_=src[:].rearrange("p (m t) -> p m t", t=PACK)[:, :, planes],
            )

        def deal_bytes(dst, src, planes):
            nc.gpsimd.tensor_copy(
                out=dst[:].rearrange("p (t m) -> p t m", t=PACK)[:, planes, :],
                in_=src[:].rearrange("p (m t) -> p t m", t=PACK)[:, planes, :],
            )

        halves = [slice(0, HALF), slice(HALF, S)]
        half_lists = [slice(0, HALF // GROUP), slice(HALF // GROUP, S // GROUP)]

        deal(w1_d, w1_w, slice(0, 4))
        nc.vector.tensor_copy(xg_s[:], x_s[:].indirect(offs_sb[:]))
        xg_w = [keep.tile([P, HALF], U32, name="xg_w%d" % a, align_bytes=64) for a in range(2)]
        for a in range(2):
            nc.vector.tensor_copy(xg_w[a][:], x_w[:].indirect(offs_sb[:, half_lists[a]]))
        w1s_d = keep.tile([P, H], U8, name="w1s_d", align_bytes=64)
        deal_bytes(w1s_d, w1_s, slice(0, 2))
        deal_bytes(w1s_d, w1_s, slice(2, 4))

        def first_product(out, t, a):
            wc = slice(t * P, (t + 1) * P)
            nc.tensor.matmul_mx(
                out=out, lhsT=w1_d[:, wc].bitcast(FP8X4), lhsT_scale=w1s_d[W1_ROW:P, wc],
                rhs=xg_w[a][:].bitcast(FP8X4), rhs_scale=xg_s[:, halves[a]], start=True, stop=True,
            )

        y_half = {t: [psum.tile([P, HALF], F32, name="y%d_%d" % (t, a), tag="y%d_%d" % (t, a)) for a in range(2)] for t in (0, 1)}
        y_whole = {t: psum.tile([P, S], F32, name="y%d" % t, tag="y%d" % t) for t in (2, 3)}
        for a in range(2):
            for t in (0, 1):
                first_product(y_half[t][a][:], t, a)
        for t in (2, 3):
            for a in range(2):
                first_product(y_whole[t][:, halves[a]], t, a)

        def plane(name):
            return keep.tile([P, S], F32, name=name, tag=name, align_bytes=64)

        def columns(name, count):
            return keep.tile([P, count], F32, name=name, tag=name, align_bytes=64)

        def fetch(name, table):
            picked = keep.tile([P, S], F32, name=name, align_bytes=64)
            nc.scalar.activation(picked[:], table[:].indirect(sty_sb[:]), ACT.Copy)
            return picked

        def look_up(out, table, a, other, op):
            nc.vector.tensor_tensor(out, table[:].indirect(sty_sb[:, half_lists[a]]), other, op)

        gain = [fetch("gain0", g_sb[0]), fetch("gain1", g_sb[1])]
        shift = [fetch("shift0", b_sb[0]), fetch("shift1", b_sb[1])]

        stats = {t: keep.tile([P, 2, 6], F32, name="stats%d" % t, align_bytes=64) for t in (0, 1)}
        for t in (2, 3):
            stats[t] = columns("stats%d" % t, 6)
        pairs = ((0, 1), (2, 3))
        moments = [keep.tile([P, 2, 2], F32, name="moments%d" % e, align_bytes=64) for e in range(2)]
        moment_of = {t: moments[e][:, i, :] for e, pair in enumerate(pairs) for i, t in enumerate(pair)}
        rstd = {}

        def mean_of(t):
            return moment_of[t][:, 0:1]

        def aggregate(t):
            src = stats[t][:].rearrange("p a s -> p (a s)") if t in y_half else stats[t][:]
            nc.vector.bn_aggr(moment_of[t], src)

        def rstd_of(e, engine, spread_tag, rstd_tag):
            spread = keep.tile([P, 2], F32, name="spread%d" % e, tag=spread_tag, align_bytes=64)
            engine.tensor_scalar(spread[:], moments[e][:, :, 1], EPS, None, ALU.add)
            both = keep.tile([P, 2], F32, name="rstd%d" % e, tag=rstd_tag, align_bytes=64)
            nc.gpsimd.tensor_tensor(both[:], spread[:], power[:], ALU.pow)
            for i, t in enumerate(pairs[e]):
                rstd[t] = both[:, i : i + 1]

        w2s_d = keep.tile([P, N], U8, name="w2s_d", align_bytes=64)
        deal_bytes(w2s_d, w2_s, slice(0, 4))
        for a in range(2):
            for t in (0, 1):
                nc.vector.bn_stats(stats[t][:, a, :], y_half[t][a][:])
        aggregate(0)
        nc.vector.bn_stats(stats[2][:], y_whole[2][:])
        aggregate(1)
        rstd_of(0, nc.gpsimd, "spread0", "rstd0")
        nc.vector.bn_stats(stats[3][:], y_whole[3][:])
        aggregate(2)

        prod = [plane("prod%d" % t) for t in range(PACK)]

        def centre_and_gain(t, a):
            nc.vector.scalar_tensor_tensor(prod[t][:, halves[a]], y_half[t][a][:], mean_of(t), gain[t][:, halves[a]], ALU.subtract, ALU.mult)

        aggregate(3)
        centre_and_gain(0, 0)
        rstd_of(1, nc.vector, "spread1", "spread0")
        centre_and_gain(0, 1)
        for a in range(2):
            centre_and_gain(1, a)

        u = keep.tile([P, PACK, S], F32, name="u", tag="u", align_bytes=64)

        def scale_and_shift(out, t, cols):
            nc.vector.scalar_tensor_tensor(out, prod[t][:, cols], rstd[t], shift[t][:, cols], ALU.mult, ALU.add)

        scale_and_shift(u[:, 0, :], 0, slice(0, S))
        late_columns = keep.tile([P, 2], F32, name="late_columns", tag="b_sb0", align_bytes=64)
        offset3, neg_rstd2 = late_columns[:, 0:1], late_columns[:, 1:2]
        nc.vector.tensor_scalar(offset3, mean_of(3), rstd[3], -1.0, ALU.mult, ALU.mult)
        nc.vector.tensor_scalar(neg_rstd2, rstd[2], -1.0, None, ALU.mult)
        scale_and_shift(u[:, 1, :], 1, slice(0, S))
        h_high = keep.tile([P, 2, S], F32, name="h_high", tag="b_sb1", align_bytes=64)
        nc.scalar.activation(h_high[:, 0, :], y_whole[2][:], ACT.Identity, bias=mean_of(2), scale=-1.0)
        nc.scalar.activation(h_high[:, 1, :], y_whole[3][:], ACT.Identity, bias=offset3, scale=rstd[3])
        shift.append(fetch("shift2", b_sb[2]))
        nc.vector.tensor_tensor(prod[2][:], g_sb[2][:].indirect(sty_sb[:]), h_high[:, 0, :], ALU.mult)
        nc.vector.tensor_tensor(prod[3][:], g_sb[3][:].indirect(sty_sb[:]), h_high[:, 1, :], ALU.mult)
        nc.vector.scalar_tensor_tensor(u[:, 2, :], prod[2][:], neg_rstd2, shift[2][:], ALU.mult, ALU.add)

        out_rows = out_0.rearrange("(p t) j -> p t j", t=PACK)
        out_words = out_1[0].rearrange("p n t -> p (n t)").bitcast(I32)
        o_s = keep.tile([P, S], U8, name="o_s", align_bytes=64)
        z_flat = keep.tile([P, S * PACK], BF16, name="z_flat", tag="b_sb2", align_bytes=64)
        z_sb = z_flat[:].rearrange("p (j t) -> p j t", t=PACK)

        def gelu(planes, first, last):
            cols = slice(first * CHUNK, last * CHUNK)
            nc.scalar.activation(z_sb[:, cols, planes], u[:, planes, cols].rearrange("p t j -> p j t"), ACT.Gelu_apprx_tanh)

        def second_product(c, bank_tags):
            z_w = keep.tile([P, CHUNK], U32, name="z_w%d" % c, tag="z_w%d" % (0, 1, 0, 3)[c], align_bytes=64)
            z_s = keep.tile([P, CHUNK], U8, name="z_s%d" % c, tag="z_s%d" % (c % 3), align_bytes=64)
            first = c * CHUNK * PACK
            nc.vector.quantize_mx(out=z_w[:].bitcast(FP8X4), scales=z_s[:], in_=z_flat[:, first : first + CHUNK * PACK])
            if c == 0:
                deal(w2_d, w2_w, slice(2, 4))
            per_bank = PACK // len(bank_tags)
            banks = [psum.tile([P, per_bank, CHUNK], F32, name="acc%d_%s" % (c, tag), tag=tag) for tag in bank_tags]
            for t in range(PACK):
                wc = slice(t * P, (t + 1) * P)
                nc.tensor.matmul_mx(
                    out=banks[t // per_bank][:, t % per_bank, :], lhsT=w2_d[:, wc].bitcast(FP8X4), lhsT_scale=w2s_d[W2_ROW:P, wc],
                    rhs=z_w[:].bitcast(FP8X4), rhs_scale=z_s[:], start=True, stop=True,
                )
            return banks

        o32 = [keep.tile([P, PACK, CHUNK], F32, name="o32_%d" % c, tag=tag, align_bytes=64)[:] for c, tag in enumerate(("o32_0", "u"))]
        o32_second = keep.tile([P, PACK, HALF], F32, name="o32_second")
        o32.extend(o32_second[:, :, c * CHUNK : (c + 1) * CHUNK] for c in range(2))
        o16 = [keep.tile([P, 2, CHUNK, PACK], BF16, name="o16_%d" % a, tag=tag, align_bytes=64) for a, tag in enumerate(("b_sb2", "o16_1"))]
        o_w = keep.tile([P, S], U32, name="o_w", align_bytes=64)

        def round_out(c):
            nc.vector.tensor_copy(o16[c // 2][:, c % 2, :, :], o32[c].rearrange("p t j -> p j t"))

        def quantise_out(a, first, count):
            cols = slice(a * HALF + first * CHUNK, a * HALF + (first + count) * CHUNK)
            nc.vector.quantize_mx(
                out=o_w[:, cols].bitcast(FP8X4), scales=o_s[:, cols],
                in_=o16[a][:, first : first + count, :, :].rearrange("p c j t -> p (c j t)"),
            )

        gelu(slice(0, 2), 0, 3)
        look_up(u[:, 3, halves[0]], b_sb[3], 0, prod[3][:, halves[0]], ALU.add)
        shift3 = keep.tile([P, HALF], F32, name="shift3", align_bytes=64)
        nc.scalar.activation(shift3[:], b_sb[3][:].indirect(sty_sb[:, half_lists[1]]), ACT.Copy)
        w2_d = keep.tile([P, N], U32, name="w2_d", align_bytes=64)
        deal(w2_d, w2_w, slice(0, 2))
        nc.vector.tensor_tensor(u[:, 3, halves[1]], prod[3][:, halves[1]], shift3[:], ALU.add)
        for c in range(3):
            gelu(slice(2, 4), c, c + 1)
        gelu(slice(0, 4), 3, 4)
        acc0 = second_product(0, ["acc0", "acc1"])
        acc1 = second_product(1, ["y2", "y3"])
        nc.vector.tensor_copy(o32[0][:, 0:2, :], acc0[0][:])
        nc.sync.dma_start(out=out_rows[:, 0:2, 0:CHUNK], in_=o32[0][:, 0:2, :])
        acc2 = second_product(2, ["y0_0", "y0_1"])
        nc.vector.tensor_copy(o32[0][:, 2:4, :], acc0[1][:])
        nc.sync.dma_start(out=out_rows[:, 2:4, 0:CHUNK], in_=o32[0][:, 2:4, :])
        acc3 = second_product(3, ["y1_0", "y1_1"])
        nc.scalar.copy(o32[1][:, 0:2, :], acc1[0][:])
        nc.vector.tensor_copy(o32[1][:, 2:4, :], acc1[1][:])
        nc.sync.dma_start(out=out_rows[:, :, CHUNK:HALF], in_=o32[1])
        for e in range(2):
            nc.scalar.copy(o32[2][:, 2 * e : 2 * e + 2, :], acc2[e][:])
        for e in range(2):
            nc.scalar.copy(o32[3][:, 2 * e : 2 * e + 2, :], acc3[e][:])
            nc.sync.dma_start(out=out_rows[:, 2 * e : 2 * e + 2, halves[1]], in_=o32_second[:, 2 * e : 2 * e + 2, :])
        for c in range(2):
            round_out(c)
        quantise_out(0, 0, 1)
        quantise_out(0, 1, 1)
        round_out(2)
        round_out(3)
        quantise_out(1, 0, 1)
        quantise_out(1, 1, 1)

        nc.scalar.dma_start(out=out_words, in_=o_w[:].bitcast(I32))
        for r in range(PACK):
            eng = nc.scalar if r % 2 else nc.sync
            eng.dma_start(out=out_2[0, r:SCALE_ROWS:PACK, :].bitcast(I32), in_=o_s[r:P:QUADRANT, :].bitcast(I32))
